import numpy as np, ml_dtypes
CORES = [2,3,42,43,82,83,122,123]
N = 8
import mx_ref
BF = ml_dtypes.bfloat16
def gcols(t, e):
    v = np.concatenate([t.reshape(8, 16, -1, 4), np.zeros((8, 16, 1, 4), BF)], axis=2)
    return np.ascontiguousarray(np.stack([v[g][:, e[g]] for g in range(8)])).reshape(128, -1)
def tile(rs):
    return np.stack(rs, axis=2).reshape(128, -1).astype(BF)
def cut(t, i, w=512):
    return t[:, w * i:w * i + w]
def pick(q, e):
    c = np.concatenate([q[0].reshape(128, -1, 4), np.zeros((128, 1, 4), np.uint8)], axis=1); s = np.concatenate([q[1], np.ones((16, 1), np.uint8)], axis=1)
    return (np.ascontiguousarray(c[:, e].reshape(128, -1)), np.ascontiguousarray(s[:, e]))
def join(*qs):
    return (np.concatenate([q[0] for q in qs], axis=1), np.concatenate([q[1] for q in qs], axis=1))
def put(q, e, v):
    c, s = q[0].reshape(128, -1, 4).copy(), q[1].copy(); c[:, e] = v[0].reshape(128, -1, 4); s[:, e] = v[1]
    return (c.reshape(128, -1), s)
def pk(c, s):
    return (np.ascontiguousarray(c), mx_ref.live(s))
def emit(q):
    return q[0], q[1]
def packed(v, rng):
    q = [mx_ref.quantize(np.ascontiguousarray(v[r])) for r in range(N)]
    return np.stack([a for a, b in q]), np.stack([mx_ref.plane(b, rng) for a, b in q])
def values_of_codes():
    e, c = np.zeros((128, 128, 4), np.float32), np.zeros((128, 2, 4), np.uint8)
    e[np.arange(128), np.arange(128), 0] = 1
    c[:127, :, 0] = np.arange(256).reshape(2, 128).T[:127]
    return mx_ref.matmul(mx_ref.quantize(e.reshape(128, 512).astype(BF)), (c.reshape(128, 8), np.full((16, 2), 127, np.uint8))).T.reshape(-1).astype(np.float64)
CODE_VALUE, SCALE_VALUE = values_of_codes(), 2.0 ** (np.arange(256) - 127.0)
def decode(q):
    return (CODE_VALUE[q[0]].reshape(16, 8, -1, 4) * SCALE_VALUE[q[1]][:, None, :, None] + 0.0).reshape(128, -1).astype(np.float32)
def f(rng, *shape):
    return mx_ref.flush((rng.standard_normal(shape, dtype=np.float32) * np.exp2(rng.integers(-2, 3, shape[:-1] + (1,)))).astype(BF))
def wide(rng, *shape, cols=0):
    v = rng.standard_normal(shape, dtype=np.float32) * np.exp2(rng.integers(-12, 13, shape)).astype(np.float32)
    if cols: v *= np.repeat(np.exp2(rng.integers(-cols, cols + 1, shape[:-2] + (1, shape[-1] // 4))) * (rng.random(shape[:-2] + (1, shape[-1] // 4)) > 0.0625), 4, axis=-1).astype(np.float32)
    return mx_ref.flush(v.astype(BF))
C = 448
def order(p):
    return np.argsort(-(p[::16] + np.float32(0.0)), axis=1, kind="stable")
def swap(qs, k, n):
    e = np.arange(1, n, 2)
    return [put(qs[r], e, pick(qs[r ^ k], e)) for r in range(N)]
def half(z):
    return mx_ref.quantize(np.ascontiguousarray((z * np.float32(0.5)).astype(BF).reshape(128, -1)))
def big(v, k):
    v = v.astype(np.float32) * np.float32(k)
    v[np.abs(v) < np.float32(2.0 ** -16)] = 0
    return v.astype(BF)
def numbers_of(rng):
    return {"x": big(f(rng, N, 128, 4 * C), 1), "ua": np.array(f(rng, N, 128, 512)), "ub": np.array(f(rng, N, 128, 512)), "v": np.array(f(rng, N, 128, 512))}
def weights(rng, w):
    c, p = packed(w, rng)
    return {"wc": c, "ws": p}
def still(rng):
    w = np.zeros((N, 128, 4, 128, 4), np.float32)
    i = np.arange(128)
    for b in range(4): w[:, i, b, i, b] = 32
    return weights(rng, w.reshape(N, 128, 2048).astype(BF))
def signs(rng):
    return np.stack([rng.permutation(8) % 2 * 2.0 - 1.0 for r in range(N)])
def setup_inputs(rng):
    return {**numbers_of(rng), **weights(rng, f(rng, N, 128, 2048))}
def setup_inputs_ties(rng):
    d = numbers_of(rng)
    e = rng.permutation(N)
    x = d["x"].reshape(N, 8, 16, C, 4)
    for r in range(N):
        k = np.zeros(C, int) if r == e[0] else rng.permutation(C) % 3
        a = x[r][:, :8, :3].copy()
        a[:, :, 2] = 0
        x[r][:, :8] = a[:, :, k]
    x[e[1]] = 0
    for n in ("ua", "ub"):
        u = d[n].reshape(N, 8, 16, 128, 4)
        u[:, :, 8:, ::16] = 0
        d[n] = u.reshape(N, 128, 512)
    w = np.array(f(rng, N, 128, 2048)).reshape(N, 8, 16, 4, 8, 16, 4)
    w[:, :, 8:, :, :, :8] = 0
    return {**d, "x": x.reshape(N, 128, 4 * C), **weights(rng, w.reshape(N, 128, 2048))}
def setup_inputs_near(rng):
    d = numbers_of(rng)
    x = np.zeros((N, 8, 16, C, 4), np.float32)
    m = np.arange(C) // 2
    x[:, :, 0, :, 0] = np.repeat(signs(rng)[::2], 2, axis=0)[:, :, None]
    for p, s in ((8, m), (10, (C // 2 - 1 - m) // 2)):
        g = ((s[:, None] >> np.arange(8)) & 1) * np.exp2(np.arange(8) - 23.0)
        x[:, :, p] = g[:, :4]
        x[:, :, p + 1] = g[:, 4:]
    x[:, :, 12:] = rng.integers(4, 8, (N, 8, 4, C, 4)) * rng.choice([-1.0, 1.0], (N, 8, 4, C, 4)) * 2.0 ** -20
    for n, p in (("ua", 8), ("ub", 10)):
        u = d[n].reshape(N, 128, 128, 4)
        u[:, :, ::16] = 0
        for h in range(0, 128, 16):
            u[:, h, h, 0] = 2.0 ** -28
            u[:, h + p:h + p + 2, h] = 2.0 ** -28
        d[n] = u.reshape(N, 128, 512)
    return {**d, "x": x.reshape(N, 128, 4 * C).astype(BF), **still(rng)}
def setup_inputs_huge(rng):
    d = numbers_of(rng)
    x = 2.0 ** 29 * (0.6 + 0.4 * rng.random((N, 128, C, 4)))
    both = np.repeat(rng.permutation(N // 2) < N // 4, 2)
    c = np.stack([rng.permutation(C) % 2 * 2.0 - 1.0 for r in range(N)])
    c[~both] = 1
    x *= c[:, None, :, None]
    g = signs(rng)
    g[both] = g[both][:, :1]
    for n, s in (("ua", g), ("ub", signs(rng))):
        u = d[n].reshape(N, 128, 128, 4)
        a = 2.0 ** 30 * (1 - 0.25 * rng.random((N, 128, 8, 4))) * s[:, None, :, None]
        u[:, :, ::16] = a.astype(np.float32).astype(BF)
        d[n] = u.reshape(N, 128, 512)
    return {**d, "x": x.astype(np.float32).reshape(N, 128, 4 * C).astype(BF), **still(rng)}
def setup_inputs_sizes(rng):
    d = setup_inputs(rng)
    k = np.concatenate([rng.permutation(4) for i in range(N // 4)]) * 5.0
    d["x"] = big(d["x"].astype(np.float32) * np.exp2(k).astype(np.float32)[:, None, None], 1)
    return d
def setup_inputs_spread(rng):
    d = setup_inputs(rng)
    d["x"] = big(wide(rng, N, 128, 4 * C, cols=6), 1)
    return d
def check_inputs(d):
    b = []
    for k in ("x", "ua", "ub", "v"):
        a = np.abs(d[k].astype(np.float32))
        if not (np.isfinite(a).all() and ((a == 0) | (a >= 2.0 ** -30) & (a <= 2.0 ** 30)).all()): b.append("a value of " + k)
    return b
def reference(x, ua, ub, v, wc, ws):
    lay = [pk(wc[r], ws[r]) for r in range(N)]
    now = [mx_ref.quantize(x[r]) for r in range(N)]
    orders, highs = [], []
    for l in range(2):
        s, n = (ua, ub)[l], C >> l
        d = decode(join(*now)).astype(BF)
        o, low, high = [], [], []
        for r in range(N):
            o.append(order(mx_ref.matmul(mx_ref.quantize(s[r]), now[r])))
            z = gcols(cut(d, r, 4 * n), o[r]).astype(np.float32).reshape(128, n // 2, 2, 4)
            low.append(half(z[:, :, 0] + z[:, :, 1]))
            high.append(half(z[:, :, 0] - z[:, :, 1]))
        orders.append(o)
        highs.append(high)
        low = swap(low, 1 << l, n // 2)
        now = [mx_ref.quantize(tile([mx_ref.matmul(pick(lay[r], np.arange(128 * b, 128 * b + 128)), low[r]) * np.float32(0.03125) for b in range(4)])) for r in range(N)]
    for l in (1, 0):
        m = C >> (l + 1)
        now = swap(now, 1 << l, m)
        d = decode(join(*now, *highs[l]))
        new = []
        for r in range(N):
            a, h = cut(d, r, 4 * m), cut(d, N + r, 4 * m)
            i = np.argsort(orders[l][r], axis=1)
            new.append(mx_ref.quantize(gcols(np.concatenate([(a + h).astype(BF), (a - h).astype(BF)], axis=1), i // 2 + m * (i % 2))))
        now = new
    y, ol = np.zeros((N, 128, C), np.float32), np.zeros((N, 8, C + C // 2), np.float32)
    oc, osc = np.zeros((N, 128, 4 * C), np.uint8), np.zeros((N, 16, C), np.uint8)
    for r in range(N):
        y[r] = mx_ref.matmul(mx_ref.quantize(v[r]), now[r])
        ol[r] = np.concatenate([orders[0][r], orders[1][r]], axis=1)
        oc[r], osc[r] = emit(now[r])
    return {"y": y, "ol": ol, "oc": oc, "osc": osc}

@@ -1,0 +1,504 @@
+from concourse.mybir import dt, AluOpType, AxisListType, ActivationFunctionType
+
+A = AluOpType
+F = ActivationFunctionType
+C = 448
+H = C // 2
+BIG = 2.0 ** 96
+STEP = 1024.0
+NV = (17, 7)
+CUT = 288
+M = (112, 64)
+BF, F32, I32, U16, Q8, U8 = "bfloat16", "float32", "int32", "uint16", "float8_e4m3fn_x4", "uint8"
+
+
+def _tiles(n):
+    segs = ["d"] + list(range(n // 16 - 1, 0, -1))
+    out = []
+    for u in range(0, len(segs), 4):
+        s = segs[u:u + 4]
+        out.append((max(128, n if u == 0 else 16 * s[0]), s))
+    return out
+
+
+def _scratch():
+    s = {}
+
+    def sb(name, cols, d):
+        s[name] = ("sbuf", [128, cols], d)
+
+    def mx(name, cols):
+        sb(name + "q", cols, Q8)
+        sb(name + "s", cols, U8)
+    sb("xt", 4 * C, BF); sb("uat", 512, BF); sb("ubt", 512, BF); sb("vt", 512, BF)
+    mx("a0", C); mx("a1", H); mx("ua_", 128); mx("ub_", 128); mx("v_", 128); mx("pa", 128); mx("pb", 128); mx("w_", 512)
+    sb("pi", 16, I32); sb("pf", 16, F32); sb("ofu", 8, U16)
+    sb("jm", C, BF); sb("one", 516, BF); sb("jj", C, F32); sb("ct", 64, F32)
+    sb("kk", 5 * C, BF)
+    sb("gt", 512, BF); sb("et", 3 * 520, BF); mx("g_", 128); mx("e_", 12 * 128)
+    sb("ms", C, F32); sb("cf", C, F32); sb("tmp", 4 * C, BF); sb("sc", 256 * 16, BF); sb("dsc", C, BF); sb("csc", C, F32)
+    sb("tr", 192, F32); sb("ii", 4 * 64, I32); sb("fi", 4 * 64, F32)
+    sb("rk", 64, F32); sb("ru", 64, U16); sb("hu", 64, U16); sb("au", 128, U16); sb("rs", 64, F32)
+    sb("a1t", 2 * C, BF); sb("a2t", 512, BF); mx("a2", 256); sb("u1t", 1024, BF); mx("u1", 240); mx("u1o", 128)
+    sb("u0t", 4 * C, BF); mx("u0", C); sb("yt", C, F32)
+    for l in range(2):
+        n = C >> l
+        w = sum(t[0] for t in _tiles(n))
+        L = str(l)
+        sb("fl" + L, 4 * w, BF); mx("fl" + L, w)
+        sb("oo" + L, 512 >> l, F32)
+        sb("lsc" + L, 4 * M[l], F32); sb("lu" + L, 32, U16); sb("dh" + L, 4 * n, BF); sb("x1" + L, 8 * M[l], BF)
+        sb("lt" + L, 1024, BF); mx("lo" + L, 128); mx("lw" + L, 128 + n // 4)
+        sb("hw" + L, 16 * M[l], BF); sb("ht" + L, 4 * n, BF); mx("h" + L, n)
+        mx("pe" + L, n); mx("po" + L, n)
+    s["ps"] = ("psum", [128, 4096], F32)
+    return s
+
+
+SCRATCH = _scratch()
+SEMAPHORES = ["V", "S", "P", "G", "sent"] + ["arr%d" % k for k in range(4)] + ["d%d" % k for k in range(24)]
+
+
+def rank_program(g, core, T, topo):
+    rank = T.rank_of(core)
+    if rank is None:
+        return
+    Q = {"V": g.vector, "S": g.scalar, "P": g.tensor, "G": g, "Y": g.sync}
+    total = {}
+    seen = {e: {} for e in Q}
+    wrote, read = {}, {}
+    ndma = [0]
+
+    def need(e, r, w):
+        want = {}
+
+        def add(sem, val, who):
+            if not (e == "P" and who == "P"):
+                want[sem] = max(want.get(sem, 0), val)
+        for t in list(r) + list(w):
+            if t in wrote:
+                add(*wrote[t])
+        for t in w:
+            for sem, (val, who) in read.get(t, {}).items():
+                add(sem, val, who)
+        for t in r:
+            if t.startswith("ps"):
+                for sem, (val, who) in read.get(t, {}).items():
+                    if who != e:
+                        add(sem, val, who)
+        for sem, val in want.items():
+            if seen[e].get(sem, 0) < val:
+                Q[e].wait_ge(T.sem[sem], val)
+                seen[e][sem] = val
+
+    def mark(sem, e, r, w):
+        for t in r:
+            read.setdefault(t, {})[sem] = (total[sem], e)
+        for t in w:
+            wrote[t] = (sem, total[sem], e)
+            read[t] = {}
+
+    def op(e, fn, r, w):
+        need(e, r, w)
+        fn().then_inc(T.sem[e], 1)
+        total[e] = total.get(e, 0) + 1
+        mark(e, e, r, w)
+
+    def dma(e, out, in_, r, w):
+        need(e, r, w)
+        sem = "d%d" % ndma[0]
+        ndma[0] += 1
+        Q[e].dma_start(out, in_).then_inc(T.sem[sem], 16)
+        total[sem] = 16
+        mark(sem, "dma", r, w)
+
+    def swap(k, l, src, dst, b, cols, r, w):
+        peer = T.cores[rank ^ (1 << l)]
+        rid, pid = topo.addr(peer)[:2]
+        m, sem = topo.mask(core, peer), "arr%d" % k
+        need("G", r, [])
+        g.remote_dma(T[dst + "q"][:, b:b + cols].bitcast(dt.uint8), T[src + "q"][:, 0:cols].bitcast(dt.uint8), T.sem[sem], T.sem.sent, pid, rid, m)
+        g.remote_dma(T[dst + "s"][:, b:b + cols], T[src + "s"][:, 0:cols], T.sem[sem], T.sem.sent, pid, rid, m)
+        total["sent"] = total.get("sent", 0) + 2 * len(topo.engines(core, peer))
+        total[sem] = 2 * len(topo.engines(peer, core))
+        mark(sem, "far", [], w)
+
+    V, S, PE = g.vector, g.scalar, g.tensor
+
+    def bank(b, a, z, step=1):
+        return T.ps[:, 512 * b + a:512 * b + z:step] if step != 1 else T.ps[:, 512 * b + a:512 * b + z]
+
+    def four(name):
+        return ["%s.%d" % (name, b) for b in range(4)]
+
+    def quant(dst, a, n, src, r, w):
+        op("V", lambda: V.quantize_mx(T[dst + "q"][:, a:a + n], T[dst + "s"][:, a:a + n], src), r, w)
+
+    def mm(b, st, sa, mv, a, n, start, stop, r):
+        op("P", lambda: PE.matmul_mx(bank(b, 0, n), T[st + "q"][:, sa:sa + 128], T[st + "s"][:, sa:sa + 128],
+                                     T[mv + "q"][:, a:a + n], T[mv + "s"][:, a:a + n], start, stop), r, ["ps%d" % b])
+
+    def ts(out, in0, s1, s2, o0, o1, r, w):
+        if s2 is None:
+            op("V", lambda: V.tensor_scalar(out, in0, s1, None, o0), r, w)
+        else:
+            op("V", lambda: V.tensor_scalar(out, in0, s1, s2, o0, o1), r, w)
+
+    def tt(out, in0, in1, o, r, w):
+        op("V", lambda: V.tensor_tensor(out, in0, in1, o), r, w)
+
+    def scan(out, d0, d1, o0, o1, r, w):
+        op("V", lambda: V.tensor_tensor_scan(out, d0, d1, 0.0, o0, o1), r, w)
+
+    def cp(out, in_, r, w):
+        op("V", lambda: V.tensor_copy(out, in_), r, w)
+
+    def fill(ap, val, w):
+        op("V", lambda: V.memset(ap, val), [], w)
+
+    def act(out, in_, f, r, w, **kw):
+        op("S", lambda: S.activation(out, in_, f, **kw), r, w)
+
+    def scaled(e, out, in_, c, r, w):
+        if e == "V":
+            if c == 1.0:
+                cp(out, in_, r, w)
+            else:
+                ts(out, in_, c, None, A.mult, None, r, w)
+        elif c == 1.0:
+            act(out, in_, F.Copy, r, w)
+        else:
+            act(out, in_, F.Copy, r, w, scale=c)
+
+    def pick(dst, a, src, lo, hi, off, n, r, w):
+        cp(T[dst + "q"][:, a:a + n].bitcast(dt.uint32), T[src + "q"][:, lo:hi].bitcast(dt.uint32).indirect(off), r, [w + "q"])
+        act(T[dst + "s"][:, a:a + n], T[src + "s"][:, lo:hi].indirect(off), F.Copy, r, [w + "s"])
+
+    def iota(out, pattern, base, cm, w, small=True):
+        if small:
+            op("G", lambda: g.iota(out, pattern, base, cm, allow_small_or_imprecise_dtypes=True), [], w)
+        else:
+            op("G", lambda: g.iota(out, pattern, base, cm), [], w)
+
+    def zero(ap, n, w):
+        iota(ap, [[0, n]], 0, 0, w)
+
+    def col(k):
+        return T.pf[:, k:k + 1]
+
+    dma("Y", T.uat[:], T.ua[:], [], ["uat"])
+    dma("S", T.xt[:, 0:4 * H], T.x[:, 0:4 * H], [], ["xt0"])
+    dma("Y", T.xt[:, 4 * H:4 * C], T.x[:, 4 * H:4 * C], [], ["xt1"])
+    dma("Y", T.ubt[:], T.ub[:], ["xt0", "xt1"], ["ubt"])
+    dma("Y", T.w_q[:].bitcast(dt.uint8), T.wc[:], [], ["wq"])
+    dma("Y", T.w_s[:], T.ws[:], [], ["wsc"])
+    dma("Y", T.vt[:], T.v[:], [], ["vt"])
+
+    iota(T.pi[:, 0:1], [[0, 1]], 0, 1, ["pi"], False)
+    iota(T.pi[:, 8:16], [[16, 8]], 0, 0, ["ofi"], False)
+    iota(T.jm[:], [[0, 28], [1, 16]], 0, 0, ["jm"])
+    fill(T.one[:], 1.0, ["one"])
+    op("G", lambda: g.affine_select(T.et[:, 0:516], T.one[:], [[1, 516]], A.is_equal, 0.0, -3, -4), ["one"], ["et0"])
+    op("G", lambda: g.affine_select(T.gt[:], T.one[:, 0:512], [[-16, 8], [0, 64]], A.is_ge, 0.0, 0, 1), ["one"], ["gt"])
+    op("G", lambda: g.affine_select(T.gt[:], T.gt[:], [[16, 8], [0, 64]], A.is_ge, 0.0, 15, -1), ["gt"], ["gt"])
+    iota(T.ct[:, 0:28], [[16, 28]], 0, 0, ["ct"])
+    iota(T.jj[:], [[1, C]], 0, 0, ["jj"])
+    ts(T.pi[:, 1:2], T.pi[:, 0:1], 15, None, A.bitwise_and, None, ["pi"], ["pj0"])
+    cp(T.ofu[:], T.pi[:, 8:16], ["ofi"], ["ofu"])
+    cp(col(0), T.pi[:, 1:2], ["pj0"], ["pf"])
+    fill(T.rs[:], 0.0, ["rs"])
+    ts(col(3), col(0), -BIG, None, A.mult, None, ["pf"], ["pf3"])
+    ts(col(4), col(0), 1.0, BIG, A.add, A.mult, ["pf"], ["pf4"])
+    ts(col(5), col(0), -15.0, STEP, A.add, A.mult, ["pf"], ["pf5"])
+    ts(col(6), col(0), -15.0, STEP - 1.0, A.add, A.mult, ["pf"], ["pf6"])
+
+    def zero_flags(l, how):
+        a = 0
+        for u, (w, s) in enumerate(_tiles(C >> l)):
+            lo = 0 if len(s) < 4 else 16 * s[-1]
+            how(T["fl%d" % l][:, 4 * (a + lo):4 * (a + w)], 4 * (w - lo), four("fl%d.%d" % (l, u)))
+            a += w
+
+    zero_flags(0, lambda ap, n, w: fill(ap, 0.0, w))
+    zero(T.rk[:], 64, ["rk0", "rk1"])
+    zero(T.lt0[:, 448:512], 64, four("lt0.0"))
+    zero(T.lt0[:, 960:1024], 64, four("lt0.1"))
+    zero(T.tr[:, 0:32], 32, ["tr1"])
+    zero_flags(1, zero)
+    zero(T.oo1[:, 224:256], 32, ["oo1"])
+    zero(T.lt1[:, 256:512], 256, four("lt1.0"))
+    zero(T.lt1[:, 768:1024], 256, four("lt1.1"))
+    zero(T.a2t[:, 224:256], 32, four("a2o"))
+    zero(T.a2t[:, 480:512], 32, four("a2e"))
+    zero(T.u1t[:, 448:512], 64, four("u1o"))
+    zero(T.u1t[:, 960:1024], 64, four("u1e"))
+    for k in (1, 2):
+        zero(T.et[:, 520 * k + 512:520 * k + 516], 4, ["et%d" % k])
+        op("G", lambda: g.affine_select(T.et[:, 520 * k:520 * k + 512], T.et[:, 0:512], [[0, 4], [1, 2], [0, 64]], A.is_equal, 0.0, 1 - k, 0),
+           ["et0"], ["et%d" % k])
+
+    mz, kr, kk, k2, k3 = [lambda n, k=k, a=0: T.kk[:, C * k + a:C * k + n] for k in range(5)]
+    act(mz(C), T.jm[:], F.Abs, ["jm", "pf3"], ["mz"], scale=BIG, bias=col(3))
+    act(kr(C), T.jm[:], F.Relu, ["jm", "pf4"], ["kr"], scale=-BIG, bias=col(4))
+    quant("ua_", 0, 128, T.uat[:], ["uat"], ["ua_"])
+    pick("pa", 0, "ua_", 0, 128, T.ofu[:], 128, ["ua_", "ofu"], "pa")
+    act(kk(C), kr(C), F.Copy, ["kr"], ["kk"], scale=-1.0)
+    act(k3(C), T.jm[:], F.Sign, ["jm"], ["k3"])
+    act(k2(C), kr(C), F.Identity, ["kr"], ["k2"], scale=-1.0, bias=STEP)
+
+    def units(kind, bs):
+        for b in bs:
+            quant("e_", 128 * (4 * kind + b), 128, T.et[:, 520 * kind + 3 - b:520 * kind + 515 - b], ["et%d" % kind], ["e%d.%d" % (kind, b)])
+
+    units(0, (2, 3))
+    quant("a0", 0, H, T.xt[:, 0:4 * H], ["xt0"], ["a0.0"])
+    quant("a0", H, H, T.xt[:, 4 * H:4 * C], ["xt1"], ["a0.1"])
+
+    def orders(l, st, atok, bv, bs, bc, bd):
+        n, L = C >> l, str(l)
+        nt, a_, z = n // 16, "a" + L, 32 * l
+        fl, rs = T["fl" + L], T.rs
+        mm(bv, st, 0, a_, 0, n, True, True, atok + [st + "q", st + "s"])
+        mm(bs, st, 0, a_, 0, n, True, True, atok + [st + "q", st + "s"])
+        if l == 0:
+            units(0, (0, 1))
+        pv, psn = "ps%d" % bv, "ps%d" % bs
+        cut = 16 * (NV[l] + 1)
+        for lo, hi, tok in ((cut, n, "b"), (0, cut, "a")):
+            tt(T.ms[:, lo:hi], bank(bv, lo, hi), mz(hi, a=lo), A.subtract, [pv, "mz"], ["ms" + tok])
+            scan(T.cf[:, lo:hi], kk(hi, a=lo), T.ms[:, lo:hi], A.add, A.max, ["kk", "ms" + tok], ["cf" + tok])
+        tiles = _tiles(n)
+        where, start, a = {}, [], 0
+        for u, (w, s) in enumerate(tiles):
+            start.append(a)
+            for k, t in enumerate(s):
+                where[t] = (u, k)
+            a += w
+
+        def slot(t, w):
+            u, k = where[t]
+            return fl[:, 4 * start[u] + k:4 * (start[u] + w):4], "fl%d.%d.%d" % (l, u, k)
+
+        def close(u):
+            w = tiles[u][0]
+            quant("fl" + L, start[u], w, fl[:, 4 * start[u]:4 * (start[u] + w)], four("fl%d.%d" % (l, u)), ["flq%d.%d" % (l, u)])
+        long_ = list(range(nt - 1, NV[l], -1))
+        for i in range(len(long_) + 1):
+            if i < len(long_):
+                t = long_[i]
+                act(T.tmp[:, C * (i % 4):C * (i % 4) + 16 * t], bank(bs, 0, 16 * t), F.Sign, [psn, "cfb"], ["tmp%d" % (i % 4)],
+                    bias=T.cf[:, 16 * t + 15:16 * t + 16], scale=-1.0)
+            if i > 0:
+                t = long_[i - 1]
+                o, tok = slot(t, 16 * t)
+                act(o, T.tmp[:, C * ((i - 1) % 4):C * ((i - 1) % 4) + 16 * t], F.Relu, ["tmp%d" % ((i - 1) % 4), "rs"],
+                    [tok, "rs%d.%d" % (l, t)], accum_out=rs[:, z + t:z + t + 1])
+        o, tok = slot("d", n)
+        tt(o, bank(bv, 0, n), T.cf[:, 0:n], A.is_le, [pv, "cfa", "cfb"], [tok])
+        short = list(range(NV[l], 0, -1))
+        ns = min(NV[l], 16)
+        mine = [u for u, (w, s) in enumerate(tiles) if all(t != "d" and t <= NV[l] for t in s)]
+        theirs = [u for u in range(len(tiles)) if u not in mine]
+        work = sum(16 * t * 1.5 + 120 for t in short) + sum(tiles[u][0] + 20 for u in mine)
+        swork = sum(32 * t + 160 for t in long_)
+        due = {u: sum(32 * t + 160 for t in long_ if t >= min(x for x in tiles[u][1] if x != "d")) / swork for u in theirs}
+        done, closed = 0.0, []
+        for b in range(4):
+            mm(bd + b, "e_", 128 * b, a_, 0, n, True, True, atok + ["e0.%d" % b])
+        for i in range(len(short) + 1):
+            if i < len(short):
+                t = short[i]
+                o, tok = slot(t, 16 * t)
+                ts(o, bank(bv, 0, 16 * t), T.cf[:, 16 * t + 15:16 * t + 16], None, A.is_lt, None, [pv, "cfa"], [tok])
+            if i == 0:
+                o, tok = slot("d", n)
+                scan(T.dsc[:, 0:n], k3(n), o, A.mult, A.add, ["k3", tok], ["dsc"])
+            else:
+                t = short[i - 1]
+                o, tok = slot(t, 16 * t)
+                if t > ns:
+                    op("V", lambda: V.tensor_reduce(rs[:, z + t:z + t + 1], o, AxisListType.X, A.add), [tok, "rs"], ["rs%d.%d" % (l, t)])
+                else:
+                    scan(T.sc[:, 256 * t - 16 * t:256 * t], o, o, A.add, A.max, [tok], ["sc%d" % t])
+                if l == 0 and i == 2:
+                    quant("g_", 0, 128, T.gt[:], ["gt"], ["g_"])
+                    ts(T.ct[:, 32:60], T.ct[:, 0:28], col(6), None, A.add, None, ["ct", "pf6"], ["cst"])
+                done += 16 * t * 1.5 + 120
+                u, k = where[t]
+                if u in mine and t == tiles[u][1][-1]:
+                    close(u)
+                    closed.append(u)
+                    done += tiles[u][0] + 20
+                for u in theirs[:-1]:
+                    if u not in closed and done / work >= due[u] and all(x == "d" or x > NV[l] or x >= t for x in tiles[u][1]):
+                        close(u)
+                        closed.append(u)
+        cp(rs[:, z + 1:z + ns + 1], T.sc[:, 255:256 * ns:256], ["sc%d" % t for t in range(1, ns + 1)] + ["rs"], ["rs%d.v" % l])
+        tt(T.fi[:, 0:nt], T.ct[:, 32:32 + nt], T.dsc[:, 15:n:16], A.subtract, ["cst", "dsc"], ["fi0"])
+        for u in theirs:
+            if u not in closed:
+                close(u)
+                closed.append(u)
+        seq = [0] + [u for u in closed if u != 0]
+        for i, u in enumerate(seq):
+            mm(bc, "g_", 0, "fl" + L, start[u], tiles[u][0], i == 0, i == len(seq) - 1, ["g_", "flq%d.%d" % (l, u)])
+        for b in range(4):
+            scaled("S", T["dh" + L][:, n * b:n * b + n], bank(bd + b, 0, n), 0.5, ["ps%d" % (bd + b)], ["dh%d.%d" % (l, b)])
+        tt(T.fi[:, 64:64 + nt], T.fi[:, 0:nt], rs[:, z:z + nt], A.subtract, ["fi0", "rs%d.v" % l] + ["rs%d.%d" % (l, t) for t in range(ns + 1, nt)], ["fi1"])
+        scan(T.csc[:, 0:n], k2(n), bank(bc, 0, n), A.add, A.max, ["k2", "ps%d" % bc], ["csc"])
+        tt(T.rk[:, z:z + nt], T.fi[:, 64:64 + nt], T.csc[:, 15:n:16], A.add, ["fi1", "csc"], ["rk" + L])
+        cp(T.ru[:, z:z + nt], T.rk[:, z:z + nt], ["rk" + L], ["ru" + L])
+        cp(T["oo" + L][:, 0:n].indirect(T.ru[:, z:z + nt]), T.jj[:, 0:n], ["ru" + L, "jj"], ["oo" + L])
+        lists(l, 0)
+        dma("Y", T.ol[0:8, l * C:l * C + n], T["oo" + L][0:128:16, 0:n], ["oo" + L], [])
+
+    def lists(l, half):
+        L, m = str(l), M[l]
+        for k in (2 * half + 1, 2 * half):
+            scan(T["lsc" + L][:, m * k:m * k + m], k2(m), T["oo" + L][:, (k + 2) % 4:4 * m:4], A.add, A.max, ["k2", "oo" + L], ["lsc%d.%d" % (l, k)])
+            ts(T["lu" + L][:, 8 * k:8 * k + m // 16], T["lsc" + L][:, m * k + 15:m * k + m:16], col(5), None, A.add, None,
+               ["lsc%d.%d" % (l, k), "pf5"], ["lu%d.%d" % (l, k)])
+
+    def member(l, k):
+        return T["lu%d" % l][:, 8 * k:8 * k + M[l] // 16]
+
+    def lows(l, half):
+        n, L, m = C >> l, str(l), M[l]
+        name = "lt%d.%d" % (l, half)
+        for b in range(4):
+            a = m * (4 * half + b)
+            act(T["x1" + L][:, a:a + m], T["dh" + L][:, n * b:n * b + n].indirect(member(l, 2 * half + 1)), F.Copy,
+                ["lu%d.%d" % (l, 2 * half + 1), "dh%d.%d" % (l, b)], ["x1%d.%d.%d" % (l, half, b)])
+        for b in range(4):
+            a = m * (4 * half + b)
+            tt(T["lt" + L][:, 512 * half + b:512 * half + 4 * m:4], T["dh" + L][:, n * b:n * b + n].indirect(member(l, 2 * half)), T["x1" + L][:, a:a + m], A.add,
+               ["lu%d.%d" % (l, 2 * half), "dh%d.%d" % (l, b), "x1%d.%d.%d" % (l, half, b)], ["%s.%d" % (name, b)])
+        quant(("lo", "lw")[half] + L, 0, 128, T["lt" + L][:, 512 * half:512 * half + 512], four(name), [("lo", "lw")[half] + L])
+
+    def layer(l, odd, b0, out, tok, by):
+        h = (C >> l) // 4
+        a = h if odd else 0
+        r = ["lw%d" % l, "wq", "wsc"] + (["land%d" % l] if odd else [])
+        for b in range(4):
+            mm(b0 + b, "w_", 128 * b, "lw%d" % l, a, 128, True, True, r)
+        lo = 128 - h if odd else 0
+        for b in range(4):
+            scaled(by[b], out(b), bank(b0 + b, lo, lo + h), 0.03125, ["ps%d" % (b0 + b)], ["%s.%d" % (tok, b)])
+
+    def highs(l):
+        n, L, m = C >> l, str(l), M[l]
+        for half in range(2):
+            for b in range(4):
+                a, z = m * (4 * half + b), m * (2 * b + 1 - half)
+                tt(T["hw" + L][:, z:z + m], T["dh" + L][:, n * b:n * b + n].indirect(member(l, 2 * half)), T["x1" + L][:, a:a + m], A.subtract,
+                   ["lu%d.%d" % (l, 2 * half), "dh%d.%d" % (l, b), "x1%d.%d.%d" % (l, half, b)], ["hw%d.%d.%d" % (l, half, b)])
+
+    def negate(l):
+        m, hw = M[l], T["hw%d" % l]
+        scaled("S", hw[:, 8 * m:16 * m], hw[:, 0:8 * m], -1.0, four("hw%d.0" % l) + four("hw%d.1" % l), ["hn%d" % l])
+
+    def high_list(l):
+        ii, fi, L = T.ii, T.fi, str(l)
+        a, z = 32 * l, 32 * l + (32 >> l)
+        cp(ii[:, a:z], T.rk[:, a:z], ["rk" + L], ["ii0" + L])
+        ts(ii[:, 192 + a:192 + z], ii[:, a:z], 1, None, A.bitwise_and, None, ["ii0" + L], ["ii3" + L])
+        ts(ii[:, 128 + a:128 + z], ii[:, a:z], 2, None, A.bitwise_and, None, ["ii0" + L], ["ii2" + L])
+        ts(ii[:, 64 + a:64 + z], ii[:, a:z], 2, None, A.arith_shift_right, None, ["ii0" + L], ["ii1" + L])
+        ts(fi[:, a:z], ii[:, 192 + a:192 + z], 8.0 * M[l], None, A.mult, None, ["ii3" + L], ["fi0"])
+        ts(fi[:, 64 + a:64 + z], ii[:, 128 + a:128 + z], M[l] / 2.0, None, A.mult, None, ["ii2" + L], ["fi1"])
+        tt(fi[:, 128 + a:128 + z], fi[:, a:z], ii[:, 64 + a:64 + z], A.add, ["fi0", "ii1" + L], ["fi2"])
+        tt(fi[:, 192 + a:192 + z], fi[:, 128 + a:128 + z], fi[:, 64 + a:64 + z], A.add, ["fi2", "fi1"], ["fi3"])
+        cp(T.hu[:, a:z], fi[:, 192 + a:192 + z], ["fi3"], ["hu" + L])
+
+    def state_list(l):
+        ii, fi, tr, L = T.ii, T.fi, T.tr, str(l)
+        a, z = 32 * l, 32 * l + (32 >> l)
+        ts(fi[:, a:z], ii[:, 128 + a:128 + z], 64.0, None, A.mult, None, ["ii2" + L], ["fi0"])
+        tt(tr[:, 0:z - a], fi[:, a:z], ii[:, 64 + a:64 + z], A.add, ["fi0", "ii1" + L], ["tr1"])
+        op("V", lambda: V.transpose(tr[:, 32:64], tr[:, 0:32]), ["tr1"], ["tr2"])
+        for k in range(4):
+            cp(tr[:, 64 + 16 * k:80 + 16 * k], tr[:, 32 + 16 * (k // 2):48 + 16 * (k // 2)], ["tr2"], ["tr3.%d" % k])
+        op("V", lambda: V.transpose(tr[:, 128:192], tr[:, 64:128]), four("tr3"), ["tr4"])
+        cp(T.au[:, 64 * l:64 * l + 64], tr[:, 128:192], ["tr4"], ["au" + L])
+
+    def signed_highs(l, a, w):
+        L, m = str(l), M[l]
+        for b in range(4):
+            act(T["ht" + L][:, 4 * a + b:4 * (a + w):4], T["hw" + L][:, 2 * m * b:2 * m * b + 10 * m].indirect(T.hu[:, 32 * l + a // 16:32 * l + (a + w) // 16]),
+                F.Copy, ["hu" + L, "hn" + L], ["ht%d.%d.%d" % (l, a, b)])
+
+    def lay_highs(l, b0, a, w):
+        quant("h%d" % l, a, w, T["ht%d" % l][:, 4 * a:4 * (a + w)], four("ht%d.%d" % (l, a)), ["h%d.%d" % (l, a)])
+        for b in range(4):
+            mm(b0 + b, "e_", 128 * b, "h%d" % l, a, w, True, False, ["h%d.%d" % (l, a), "e0.%d" % b])
+
+    def put_back(l, b0, a, w, src, lo, hi, r):
+        for k, name in enumerate(("pe", "po")):
+            o = 64 * l + 32 * k
+            pick("%s%d" % (name, l), a, src, lo, hi, T.au[:, o + a // 16:o + (a + w) // 16], w, r + ["au%d" % l], "%s%d.%d" % (name, l, a))
+        for k, name in enumerate(("pe", "po")):
+            for b in range(4):
+                mm(b0 + b, "e_", 128 * (4 + 4 * k + b), "%s%d" % (name, l), a, w, False, k == 1,
+                   ["%s%d.%dq" % (name, l, a), "%s%d.%ds" % (name, l, a), "e%d.%d" % (k + 1, b)])
+
+    parts = ((0, CUT), (CUT, C - CUT))
+    orders(0, "pa", ["a0.0", "a0.1"], 0, 1, 2, 4)
+    lows(0, 0)
+    swap(0, 0, "lo0", "lw0", 128, 112, ["lo0"], ["land0"])
+    lists(0, 1)
+    lows(0, 1)
+    layer(0, False, 4, lambda b: T.a1t[:, b:4 * H:8], "a1e", "SSSS")
+    quant("ub_", 0, 128, T.ubt[:], ["ubt"], ["ub_"])
+    pick("pb", 0, "ub_", 0, 128, T.ofu[:], 128, ["ub_", "ofu"], "pb")
+    highs(0)
+    layer(0, True, 0, lambda b: T.a1t[:, 4 + b:4 * H:8], "a1o", "SVSV")
+    quant("a1", 0, H, T.a1t[:], four("a1e") + four("a1o"), ["a1"])
+    orders(1, "pb", ["a1"], 4, 5, 6, 0)
+    lows(1, 0)
+    swap(1, 1, "lo1", "lw1", 128, 56, ["lo1"], ["land1"])
+    lists(1, 1)
+    lows(1, 1)
+    layer(1, False, 4, lambda b: T.a2t[:, 256 + b:256 + 224:4], "a2e", "SSSS")
+    negate(0)
+    highs(1)
+    negate(1)
+    high_list(1)
+    signed_highs(1, 0, H)
+    layer(1, True, 0, lambda b: T.a2t[:, b:224:4], "a2o", "VVVV")
+    quant("a2", 0, 128, T.a2t[:], four("a2e") + four("a2o"), ["a2"])
+    swap(2, 1, "a2", "a2", 192, 56, ["a2"], ["land2"])
+    high_list(0)
+    signed_highs(0, *parts[0])
+    lay_highs(1, 4, 0, H)
+    state_list(1)
+    units(1, range(4))
+    units(2, range(4))
+    put_back(1, 4, 0, H, "a2", 64, 256, ["a2", "land2"])
+    for b in range(4):
+        scaled("VS"[b % 2], T.u1t[:, b:448:4], bank(4 + b, 1, H, 2), 1.0, ["ps%d" % (4 + b)], ["u1o.%d" % b])
+    quant("u1o", 0, 128, T.u1t[:, 0:512], four("u1o"), ["u1o"])
+    swap(3, 0, "u1o", "u1", 128, 112, ["u1o"], ["land3"])
+    signed_highs(0, *parts[1])
+    for b in range(4):
+        scaled("VS"[b // 2], T.u1t[:, 512 + b:512 + 448:4], bank(4 + b, 0, H, 2), 1.0, ["ps%d" % (4 + b)], ["u1e.%d" % b])
+    state_list(0)
+    lay_highs(0, 0, *parts[0])
+    quant("u1", 0, 128, T.u1t[:, 512:1024], four("u1e"), ["u1"])
+    lay_highs(0, 4, *parts[1])
+    quant("v_", 0, 128, T.vt[:], ["vt"], ["v_"])
+    for h, (a, w) in enumerate(parts):
+        put_back(0, 4 * h, a, w, "u1", 0, 240, ["u1", "land3"])
+    for h, (a, w) in enumerate(parts):
+        for b in range(4):
+            scaled("VS"[b % 2], T.u0t[:, 4 * a + b:4 * (a + w):4], bank(4 * h + b, 0, w), 1.0, ["ps%d" % (4 * h + b)], ["u0t.%d.%d" % (h, b)])
+        quant("u0", a, w, T.u0t[:, 4 * a:4 * (a + w)], four("u0t.%d" % h), ["u0.%d" % h])
+        mm(4 * h, "v_", 0, "u0", a, w, True, True, ["v_", "u0.%d" % h])
+        dma("Y", T.oc[:, 4 * a:4 * (a + w)], T.u0q[:, a:a + w].bitcast(dt.uint8), ["u0.%d" % h], [])
+        if h == 1:
+            for k in range(4):
+                dma("Y", T.osc[4 * k:4 * k + 4, 0:C], T.u0s[32 * k:32 * k + 4, 0:C], ["u0.0", "u0.1"], [])
+    for h, (a, w) in enumerate(parts):
+        scaled("S", T.yt[:, a:a + w], bank(4 * h, 0, w), 1.0, ["ps%d" % (4 * h)], ["yt%d" % h])
+        dma("S", T.y[:, a:a + w], T.yt[:, a:a + w], ["yt%d" % h], [])
+    for sem, val in total.items():
+        g.wait_ge(T.sem[sem], val)

@@ -32,13 +32,13 @@ def _scratch():
         sb(name + "s", cols, U8)
     sb("xt", 4 * C, BF); sb("uat", 512, BF); sb("ubt", 512, BF); sb("vt", 512, BF)
     mx("a0", C); mx("a1", H); mx("ua_", 128); mx("ub_", 128); mx("v_", 128); mx("pa", 128); mx("pb", 128); mx("w_", 512)
-    sb("pi", 16, I32); sb("pf", 16, F32); sb("ofu", 8, U16)
+    sb("pi", 24, I32); sb("pf", 16, F32); sb("ofu", 16, U16)
     sb("jm", C, BF); sb("one", 516, BF); sb("jj", C, F32); sb("ct", 64, F32)
     sb("kk", 5 * C, BF)
     sb("gt", 512, BF); sb("et", 3 * 520, BF); mx("g_", 128); mx("e_", 12 * 128)
     sb("ms", C, F32); sb("cf", C, F32); sb("tmp", 4 * C, BF); sb("sc", 256 * 16, BF); sb("dsc", C, BF); sb("csc", C, F32)
-    sb("tr", 192, F32); sb("ii", 4 * 64, I32); sb("fi", 4 * 64, F32)
-    sb("rk", 64, F32); sb("ru", 64, U16); sb("hu", 64, U16); sb("au", 128, U16); sb("rs", 64, F32)
+    sb("tr", 384, F32); sb("ii", 3 * 64, I32); sb("fi", 2 * 64, F32)
+    sb("rk", 64, F32); sb("ru", 64, U16); sb("au", 128, U16); sb("rs", 64, F32)
     sb("a1t", 2 * C, BF); sb("a2t", 512, BF); mx("a2", 256); sb("u1t", 1024, BF); mx("u1", 240); mx("u1o", 128)
     sb("u0t", 4 * C, BF); mx("u0", C); sb("yt", C, F32)
     for l in range(2):
@@ -202,9 +202,10 @@ def rank_program(g, core, T, topo):
     op("G", lambda: g.affine_select(T.gt[:], T.one[:, 0:512], [[-16, 8], [0, 64]], A.is_ge, 0.0, 0, 1), ["one"], ["gt"])
     op("G", lambda: g.affine_select(T.gt[:], T.gt[:], [[16, 8], [0, 64]], A.is_ge, 0.0, 15, -1), ["gt"], ["gt"])
     iota(T.ct[:, 0:28], [[16, 28]], 0, 0, ["ct"])
+    iota(T.pi[:, 16:24], [[16, 4], [0, 2]], 0, 0, ["dbi"], False)
     iota(T.jj[:], [[1, C]], 0, 0, ["jj"])
     ts(T.pi[:, 1:2], T.pi[:, 0:1], 15, None, A.bitwise_and, None, ["pi"], ["pj0"])
-    cp(T.ofu[:], T.pi[:, 8:16], ["ofi"], ["ofu"])
+    cp(T.ofu[:, 0:8], T.pi[:, 8:16], ["ofi"], ["ofu"])
     cp(col(0), T.pi[:, 1:2], ["pj0"], ["pf"])
     fill(T.rs[:], 0.0, ["rs"])
     ts(col(3), col(0), -BIG, None, A.mult, None, ["pf"], ["pf3"])
@@ -223,7 +224,6 @@ def rank_program(g, core, T, topo):
     zero(T.rk[:], 64, ["rk0", "rk1"])
     zero(T.lt0[:, 448:512], 64, four("lt0.0"))
     zero(T.lt0[:, 960:1024], 64, four("lt0.1"))
-    zero(T.tr[:, 0:32], 32, ["tr1"])
     zero_flags(1, zero)
     zero(T.oo1[:, 224:256], 32, ["oo1"])
     zero(T.lt1[:, 256:512], 256, four("lt1.0"))
@@ -241,7 +241,7 @@ def rank_program(g, core, T, topo):
     act(mz(C), T.jm[:], F.Abs, ["jm", "pf3"], ["mz"], scale=BIG, bias=col(3))
     act(kr(C), T.jm[:], F.Relu, ["jm", "pf4"], ["kr"], scale=-BIG, bias=col(4))
     quant("ua_", 0, 128, T.uat[:], ["uat"], ["ua_"])
-    pick("pa", 0, "ua_", 0, 128, T.ofu[:], 128, ["ua_", "ofu"], "pa")
+    pick("pa", 0, "ua_", 0, 128, T.ofu[:, 0:8], 128, ["ua_", "ofu"], "pa")
     act(kk(C), kr(C), F.Copy, ["kr"], ["kk"], scale=-1.0)
     act(k3(C), T.jm[:], F.Sign, ["jm"], ["k3"])
     act(k2(C), kr(C), F.Identity, ["kr"], ["k2"], scale=-1.0, bias=STEP)
@@ -260,8 +260,7 @@ def rank_program(g, core, T, topo):
         fl, rs = T["fl" + L], T.rs
         mm(bv, st, 0, a_, 0, n, True, True, atok + [st + "q", st + "s"])
         mm(bs, st, 0, a_, 0, n, True, True, atok + [st + "q", st + "s"])
-        if l == 0:
-            units(0, (0, 1))
+        units(l, (0, 1))
         pv, psn = "ps%d" % bv, "ps%d" % bs
         cut = 16 * (NV[l] + 1)
         for lo, hi, tok in ((cut, n, "b"), (0, cut, "a")):
@@ -345,6 +344,11 @@ def rank_program(g, core, T, topo):
         for b in range(4):
             scaled("S", T["dh" + L][:, n * b:n * b + n], bank(bd + b, 0, n), 0.5, ["ps%d" % (bd + b)], ["dh%d.%d" % (l, b)])
         tt(T.fi[:, 64:64 + nt], T.fi[:, 0:nt], rs[:, z:z + nt], A.subtract, ["fi0", "rs%d.v" % l] + ["rs%d.%d" % (l, t) for t in range(ns + 1, nt)], ["fi1"])
+        if l == 0:
+            quant("ub_", 0, 128, T.ubt[:], ["ubt"], ["ub_"])
+        else:
+            units(1, (2,))
+            negate(0)
         scan(T.csc[:, 0:n], k2(n), bank(bc, 0, n), A.add, A.max, ["k2", "ps%d" % bc], ["csc"])
         tt(T.rk[:, z:z + nt], T.fi[:, 64:64 + nt], T.csc[:, 15:n:16], A.add, ["fi1", "csc"], ["rk" + L])
         cp(T.ru[:, z:z + nt], T.rk[:, z:z + nt], ["rk" + L], ["ru" + L])
@@ -389,43 +393,32 @@ def rank_program(g, core, T, topo):
         n, L, m = C >> l, str(l), M[l]
         for half in range(2):
             for b in range(4):
-                a, z = m * (4 * half + b), m * (2 * b + 1 - half)
-                tt(T["hw" + L][:, z:z + m], T["dh" + L][:, n * b:n * b + n].indirect(member(l, 2 * half)), T["x1" + L][:, a:a + m], A.subtract,
+                a, z = m * (4 * half + b), 4 * m * b
+                tt(T["hw" + L][:, z + 2 - 2 * half:z + 4 * m:4], T["dh" + L][:, n * b:n * b + n].indirect(member(l, 2 * half)), T["x1" + L][:, a:a + m], A.subtract,
                    ["lu%d.%d" % (l, 2 * half), "dh%d.%d" % (l, b), "x1%d.%d.%d" % (l, half, b)], ["hw%d.%d.%d" % (l, half, b)])
 
     def negate(l):
         m, hw = M[l], T["hw%d" % l]
-        scaled("S", hw[:, 8 * m:16 * m], hw[:, 0:8 * m], -1.0, four("hw%d.0" % l) + four("hw%d.1" % l), ["hn%d" % l])
+        scaled("S", hw[:, 1:16 * m:2], hw[:, 0:16 * m:2], -1.0, four("hw%d.0" % l) + four("hw%d.1" % l), ["hn%d" % l])
 
-    def high_list(l):
-        ii, fi, L = T.ii, T.fi, str(l)
-        a, z = 32 * l, 32 * l + (32 >> l)
-        cp(ii[:, a:z], T.rk[:, a:z], ["rk" + L], ["ii0" + L])
-        ts(ii[:, 192 + a:192 + z], ii[:, a:z], 1, None, A.bitwise_and, None, ["ii0" + L], ["ii3" + L])
-        ts(ii[:, 128 + a:128 + z], ii[:, a:z], 2, None, A.bitwise_and, None, ["ii0" + L], ["ii2" + L])
-        ts(ii[:, 64 + a:64 + z], ii[:, a:z], 2, None, A.arith_shift_right, None, ["ii0" + L], ["ii1" + L])
-        ts(fi[:, a:z], ii[:, 192 + a:192 + z], 8.0 * M[l], None, A.mult, None, ["ii3" + L], ["fi0"])
-        ts(fi[:, 64 + a:64 + z], ii[:, 128 + a:128 + z], M[l] / 2.0, None, A.mult, None, ["ii2" + L], ["fi1"])
-        tt(fi[:, 128 + a:128 + z], fi[:, a:z], ii[:, 64 + a:64 + z], A.add, ["fi0", "ii1" + L], ["fi2"])
-        tt(fi[:, 192 + a:192 + z], fi[:, 128 + a:128 + z], fi[:, 64 + a:64 + z], A.add, ["fi2", "fi1"], ["fi3"])
-        cp(T.hu[:, a:z], fi[:, 192 + a:192 + z], ["fi3"], ["hu" + L])
-
-    def state_list(l):
-        ii, fi, tr, L = T.ii, T.fi, T.tr, str(l)
-        a, z = 32 * l, 32 * l + (32 >> l)
-        ts(fi[:, a:z], ii[:, 128 + a:128 + z], 64.0, None, A.mult, None, ["ii2" + L], ["fi0"])
-        tt(tr[:, 0:z - a], fi[:, a:z], ii[:, 64 + a:64 + z], A.add, ["fi0", "ii1" + L], ["tr1"])
-        op("V", lambda: V.transpose(tr[:, 32:64], tr[:, 0:32]), ["tr1"], ["tr2"])
-        for k in range(4):
-            cp(tr[:, 64 + 16 * k:80 + 16 * k], tr[:, 32 + 16 * (k // 2):48 + 16 * (k // 2)], ["tr2"], ["tr3.%d" % k])
-        op("V", lambda: V.transpose(tr[:, 128:192], tr[:, 64:128]), four("tr3"), ["tr4"])
-        cp(T.au[:, 64 * l:64 * l + 64], tr[:, 128:192], ["tr4"], ["au" + L])
+    def state_lists():
+        ii, fi, tr = T.ii, T.fi, T.tr
+        cp(ii[:, 0:64], T.rk[:], ["rk0", "rk1"], ["ii0"])
+        ts(T.ofu[:, 8:16], T.pi[:, 16:24], col(0), None, A.add, None, ["dbi", "pf"], ["dbu"])
+        ts(ii[:, 128:192], ii[:, 0:64], 2, None, A.bitwise_and, None, ["ii0"], ["ii2"])
+        ts(ii[:, 64:128], ii[:, 0:64], 2, None, A.arith_shift_right, None, ["ii0"], ["ii1"])
+        ts(fi[:, 0:64], ii[:, 128:192], 64.0, None, A.mult, None, ["ii2"], ["fi0"])
+        tt(tr[:, 0:64], fi[:, 0:64], ii[:, 64:128], A.add, ["fi0", "ii1"], ["tr1"])
+        op("V", lambda: V.transpose(tr[:, 64:128], tr[:, 0:64]), ["tr1"], ["tr2"])
+        cp(tr[:, 128:256], tr[:, 64:128].indirect(T.ofu[:, 8:16]), ["tr2", "dbu"], ["tr3"])
+        op("V", lambda: V.transpose(tr[:, 256:384], tr[:, 128:256]), ["tr3"], ["tr4"])
+        cp(T.au[:], tr[:, 256:384], ["tr4"], ["au"])
 
     def signed_highs(l, a, w):
         L, m = str(l), M[l]
         for b in range(4):
-            act(T["ht" + L][:, 4 * a + b:4 * (a + w):4], T["hw" + L][:, 2 * m * b:2 * m * b + 10 * m].indirect(T.hu[:, 32 * l + a // 16:32 * l + (a + w) // 16]),
-                F.Copy, ["hu" + L, "hn" + L], ["ht%d.%d.%d" % (l, a, b)])
+            act(T["ht" + L][:, 4 * a + b:4 * (a + w):4], T["hw" + L][:, 4 * m * b:4 * m * (b + 1)].indirect(T.ru[:, 32 * l + a // 16:32 * l + (a + w) // 16]),
+                F.Copy, ["ru" + L, "hn" + L], ["ht%d.%d.%d" % (l, a, b)])
 
     def lay_highs(l, b0, a, w):
         quant("h%d" % l, a, w, T["ht%d" % l][:, 4 * a:4 * (a + w)], four("ht%d.%d" % (l, a)), ["h%d.%d" % (l, a)])
@@ -435,7 +428,7 @@ def rank_program(g, core, T, topo):
     def put_back(l, b0, a, w, src, lo, hi, r):
         for k, name in enumerate(("pe", "po")):
             o = 64 * l + 32 * k
-            pick("%s%d" % (name, l), a, src, lo, hi, T.au[:, o + a // 16:o + (a + w) // 16], w, r + ["au%d" % l], "%s%d.%d" % (name, l, a))
+            pick("%s%d" % (name, l), a, src, lo, hi, T.au[:, o + a // 16:o + (a + w) // 16], w, r + ["au"], "%s%d.%d" % (name, l, a))
         for k, name in enumerate(("pe", "po")):
             for b in range(4):
                 mm(b0 + b, "e_", 128 * (4 + 4 * k + b), "%s%d" % (name, l), a, w, False, k == 1,
@@ -448,10 +441,9 @@ def rank_program(g, core, T, topo):
     lists(0, 1)
     lows(0, 1)
     layer(0, False, 4, lambda b: T.a1t[:, b:4 * H:8], "a1e", "SSSS")
-    quant("ub_", 0, 128, T.ubt[:], ["ubt"], ["ub_"])
-    pick("pb", 0, "ub_", 0, 128, T.ofu[:], 128, ["ub_", "ofu"], "pb")
+    pick("pb", 0, "ub_", 0, 128, T.ofu[:, 0:8], 128, ["ub_", "ofu"], "pb")
     highs(0)
-    layer(0, True, 0, lambda b: T.a1t[:, 4 + b:4 * H:8], "a1o", "SVSV")
+    layer(0, True, 0, lambda b: T.a1t[:, 4 + b:4 * H:8], "a1o", "SSSV")
     quant("a1", 0, H, T.a1t[:], four("a1e") + four("a1o"), ["a1"])
     orders(1, "pb", ["a1"], 4, 5, 6, 0)
     lows(1, 0)
@@ -459,33 +451,29 @@ def rank_program(g, core, T, topo):
     lists(1, 1)
     lows(1, 1)
     layer(1, False, 4, lambda b: T.a2t[:, 256 + b:256 + 224:4], "a2e", "SSSS")
-    negate(0)
     highs(1)
     negate(1)
-    high_list(1)
     signed_highs(1, 0, H)
     layer(1, True, 0, lambda b: T.a2t[:, b:224:4], "a2o", "VVVV")
     quant("a2", 0, 128, T.a2t[:], four("a2e") + four("a2o"), ["a2"])
     swap(2, 1, "a2", "a2", 192, 56, ["a2"], ["land2"])
-    high_list(0)
-    signed_highs(0, *parts[0])
+    state_lists()
     lay_highs(1, 4, 0, H)
-    state_list(1)
-    units(1, range(4))
+    signed_highs(0, *parts[1])
+    units(1, (3,))
     units(2, range(4))
     put_back(1, 4, 0, H, "a2", 64, 256, ["a2", "land2"])
+    quant("v_", 0, 128, T.vt[:], ["vt"], ["v_"])
     for b in range(4):
         scaled("VS"[b % 2], T.u1t[:, b:448:4], bank(4 + b, 1, H, 2), 1.0, ["ps%d" % (4 + b)], ["u1o.%d" % b])
     quant("u1o", 0, 128, T.u1t[:, 0:512], four("u1o"), ["u1o"])
     swap(3, 0, "u1o", "u1", 128, 112, ["u1o"], ["land3"])
-    signed_highs(0, *parts[1])
+    signed_highs(0, *parts[0])
     for b in range(4):
-        scaled("VS"[b // 2], T.u1t[:, 512 + b:512 + 448:4], bank(4 + b, 0, H, 2), 1.0, ["ps%d" % (4 + b)], ["u1e.%d" % b])
-    state_list(0)
-    lay_highs(0, 0, *parts[0])
+        scaled("V", T.u1t[:, 512 + b:512 + 448:4], bank(4 + b, 0, H, 2), 1.0, ["ps%d" % (4 + b)], ["u1e.%d" % b])
     quant("u1", 0, 128, T.u1t[:, 512:1024], four("u1e"), ["u1"])
     lay_highs(0, 4, *parts[1])
-    quant("v_", 0, 128, T.vt[:], ["vt"], ["v_"])
+    lay_highs(0, 0, *parts[0])
     for h, (a, w) in enumerate(parts):
         put_back(0, 4 * h, a, w, "u1", 0, 240, ["u1", "land3"])
     for h, (a, w) in enumerate(parts):

@@ -1,4 +1,4 @@
-from concourse.mybir import dt, AluOpType, AxisListType, ActivationFunctionType
+from concourse.mybir import dt, AluOpType, ActivationFunctionType
 
 A = AluOpType
 F = ActivationFunctionType
@@ -6,10 +6,18 @@ C = 448
 H = C // 2
 BIG = 2.0 ** 96
 STEP = 1024.0
-NV = (17, 7)
-CUT = 288
-M = (112, 64)
+LOW = -224.0
+HW = (224, 128)
+HA = (0, 16)
 BF, F32, I32, U16, Q8, U8 = "bfloat16", "float32", "int32", "uint16", "float8_e4m3fn_x4", "uint8"
+CFG = {
+    "rows": (([13, 12, 11], [21, 20, 19, 18, 17], [10, 9, 8, 7, 6, 5, 4, 3, 2]), ([], [6, 5], [9, 8, 7, 4, 3, 2])),
+    "plan": ("d c27 e c26 r s27 c25 s26 c24 s25 c23 q0 s24 c22 s23 c16 s22 c15 s16 c14 s15 q1 c1 s14 q3 s1 q2 q4 q5 q6 a b x X",
+             "d c13 e c12 r s13 c11 s12 c10 s11 c1 q0 s10 s1 q1 q2 q3 b a x X"),
+    "lows": ((0, 10, 20, 28), (0, 8, 14)),
+    "highs": (0, 20, 36, 56),
+    "parts": ((224, 112), (224, 96)),
+}
 
 
 def _tiles(n):
@@ -32,25 +40,24 @@ def _scratch():
         sb(name + "s", cols, U8)
     sb("xt", 4 * C, BF); sb("uat", 512, BF); sb("ubt", 512, BF); sb("vt", 512, BF)
     mx("a0", C); mx("a1", H); mx("ua_", 128); mx("ub_", 128); mx("v_", 128); mx("pa", 128); mx("pb", 128); mx("w_", 512)
-    sb("pi", 24, I32); sb("pf", 16, F32); sb("ofu", 16, U16)
-    sb("jm", C, BF); sb("one", 516, BF); sb("jj", C, F32); sb("ct", 64, F32)
-    sb("kk", 5 * C, BF)
-    sb("gt", 512, BF); sb("et", 3 * 520, BF); mx("g_", 128); mx("e_", 12 * 128)
-    sb("ms", C, F32); sb("cf", C, F32); sb("tmp", 4 * C, BF); sb("sc", 256 * 16, BF); sb("dsc", C, BF); sb("csc", C, F32)
-    sb("tr", 384, F32); sb("ii", 3 * 64, I32); sb("fi", 2 * 64, F32)
-    sb("rk", 64, F32); sb("ru", 64, U16); sb("au", 128, U16); sb("rs", 64, F32)
-    sb("a1t", 2 * C, BF); sb("a2t", 512, BF); mx("a2", 256); sb("u1t", 1024, BF); mx("u1", 240); mx("u1o", 128)
+    sb("pi", 16, I32); sb("pf", 16, F32); sb("ofu", 8, U16)
+    sb("jm", H, BF); sb("jn", 128, BF); sb("jq", 3 * H, BF); sb("one", 512, BF); sb("jj", C, F32); sb("ct", 64, F32)
+    sb("kk", 4 * H + C, BF)
+    sb("gt", 512, BF); sb("et", 2 * 520, BF); mx("g_", 128); mx("e_", 6 * 128)
+    sb("ms", C, F32); sb("cf", C, F32); sb("tmp", 4 * C, BF); sb("dsc", C, BF); sb("csc", C, F32)
+    sb("rk", 64, F32); sb("ru", 64, U16); sb("rs", 64, F32)
+    sb("a1t", 2 * C, BF); sb("a2t", 1024, BF); mx("a2", 184); mx("a2o", 128)
+    sb("u1t", 1024, BF); mx("u1", 240); mx("u1o", 128)
     sb("u0t", 4 * C, BF); mx("u0", C); sb("yt", C, F32)
     for l in range(2):
         n = C >> l
         w = sum(t[0] for t in _tiles(n))
         L = str(l)
-        sb("fl" + L, 4 * w, BF); mx("fl" + L, w)
-        sb("oo" + L, 512 >> l, F32)
-        sb("lsc" + L, 4 * M[l], F32); sb("lu" + L, 32, U16); sb("dh" + L, 4 * n, BF); sb("x1" + L, 8 * M[l], BF)
+        sb("fl" + L, 4 * w, BF); mx("fl" + L, w); sb("sc" + L, n // 2 * (n // 16), BF)
+        sb("oo" + L, n, F32); sb("lsc" + L, n, F32); sb("lu" + L, n // 4, U16); sb("dh" + L, 4 * n, BF); sb("x1" + L, 2 * n, BF)
         sb("lt" + L, 1024, BF); mx("lo" + L, 128); mx("lw" + L, 128 + n // 4)
-        sb("hw" + L, 16 * M[l], BF); sb("ht" + L, 4 * n, BF); mx("h" + L, n)
-        mx("pe" + L, n); mx("po" + L, n)
+        sb("ht" + L, 4 * HW[l], BF); mx("h" + L, HW[l]); sb("hd" + L, 2 * HW[l], BF); sb("wn" + L, 4 * n, BF)
+        sb("pr" + L, n, F32); sb("psc" + L, n, F32); sb("pu" + L, n // 4, U16)
     s["ps"] = ("psum", [128, 4096], F32)
     return s
 
@@ -125,8 +132,8 @@ def rank_program(g, core, T, topo):
 
     V, S, PE = g.vector, g.scalar, g.tensor
 
-    def bank(b, a, z, step=1):
-        return T.ps[:, 512 * b + a:512 * b + z:step] if step != 1 else T.ps[:, 512 * b + a:512 * b + z]
+    def bank(b, a, z):
+        return T.ps[:, 512 * b + a:512 * b + z]
 
     def four(name):
         return ["%s.%d" % (name, b) for b in range(4)]
@@ -147,8 +154,8 @@ def rank_program(g, core, T, topo):
     def tt(out, in0, in1, o, r, w):
         op("V", lambda: V.tensor_tensor(out, in0, in1, o), r, w)
 
-    def scan(out, d0, d1, o0, o1, r, w):
-        op("V", lambda: V.tensor_tensor_scan(out, d0, d1, 0.0, o0, o1), r, w)
+    def scan(out, d0, d1, o0, o1, r, w, first=0.0):
+        op("V", lambda: V.tensor_tensor_scan(out, d0, d1, first, o0, o1), r, w)
 
     def cp(out, in_, r, w):
         op("V", lambda: V.tensor_copy(out, in_), r, w)
@@ -186,6 +193,25 @@ def rank_program(g, core, T, topo):
     def col(k):
         return T.pf[:, k:k + 1]
 
+    def slots(l, u):
+        return four("fl%d.%d" % (l, u)) + (["fl0.0.4"] if l == 0 and u == 0 else [])
+
+    def zero_flags(l, us, how):
+        a = 0
+        for u, (w, s) in enumerate(_tiles(C >> l)):
+            lo = 0 if len(s) < 4 else 16 * s[-1]
+            if u in us:
+                how(T["fl%d" % l][:, 4 * (a + lo):4 * (a + w)], 4 * (w - lo), slots(l, u))
+            a += w
+
+    def ends(l):
+        h = C >> (l + 1)
+        return T["sc%d" % l][:, h - 1:h * (h // 8):h]
+
+    def units(kind, bs):
+        for b in bs:
+            quant("e_", 128 * (2 * kind + b), 128, T.et[:, 520 * kind + 3 - b:520 * kind + 515 - b], ["et%d" % kind], ["e%d.%d" % (kind, b)])
+
     dma("Y", T.uat[:], T.ua[:], [], ["uat"])
     dma("S", T.xt[:, 0:4 * H], T.x[:, 0:4 * H], [], ["xt0"])
     dma("Y", T.xt[:, 4 * H:4 * C], T.x[:, 4 * H:4 * C], [], ["xt1"])
@@ -195,77 +221,71 @@ def rank_program(g, core, T, topo):
     dma("Y", T.vt[:], T.v[:], [], ["vt"])
 
     iota(T.pi[:, 0:1], [[0, 1]], 0, 1, ["pi"], False)
+    iota(T.jn[:], [[1, 128]], 0, 0, ["jn"])
     iota(T.pi[:, 8:16], [[16, 8]], 0, 0, ["ofi"], False)
-    iota(T.jm[:], [[0, 28], [1, 16]], 0, 0, ["jm"])
+    iota(T.jm[:], [[0, H // 16], [1, 16]], 0, 0, ["jm"])
     fill(T.one[:], 1.0, ["one"])
-    op("G", lambda: g.affine_select(T.et[:, 0:516], T.one[:], [[1, 516]], A.is_equal, 0.0, -3, -4), ["one"], ["et0"])
-    op("G", lambda: g.affine_select(T.gt[:], T.one[:, 0:512], [[-16, 8], [0, 64]], A.is_ge, 0.0, 0, 1), ["one"], ["gt"])
+    iota(T.ct[:, 0:28], [[16, 28]], int(LOW), 0, ["ct"])
+    op("G", lambda: g.affine_select(T.gt[:], T.one[:], [[-16, 8], [0, 64]], A.is_ge, 0.0, 0, 1), ["one"], ["gt"])
     op("G", lambda: g.affine_select(T.gt[:], T.gt[:], [[16, 8], [0, 64]], A.is_ge, 0.0, 15, -1), ["gt"], ["gt"])
-    iota(T.ct[:, 0:28], [[16, 28]], 0, 0, ["ct"])
-    iota(T.pi[:, 16:24], [[16, 4], [0, 2]], 0, 0, ["dbi"], False)
     iota(T.jj[:], [[1, C]], 0, 0, ["jj"])
+    iota(T.jq[:, 0:H], [[0, H // 4], [1, 4]], 0, 0, ["jq"])
+
+    def wipe(ap, n, w):
+        act(ap, T.one[:, 0:n], F.Copy, ["one"], w, scale=0.0)
+
+    zero_flags(0, (3, 4, 0, 2), wipe)
     ts(T.pi[:, 1:2], T.pi[:, 0:1], 15, None, A.bitwise_and, None, ["pi"], ["pj0"])
-    cp(T.ofu[:, 0:8], T.pi[:, 8:16], ["ofi"], ["ofu"])
+    fill(T.et[:, 0:516], 0.0, ["et0"])
     cp(col(0), T.pi[:, 1:2], ["pj0"], ["pf"])
-    fill(T.rs[:], 0.0, ["rs"])
+    cp(col(1), T.pi[:, 0:1], ["pi"], ["pf1"])
     ts(col(3), col(0), -BIG, None, A.mult, None, ["pf"], ["pf3"])
+    ts(T.et[:, 3:515:4], T.jn[:], col(1), None, A.is_equal, None, ["jn", "pf1"], ["et0"])
     ts(col(4), col(0), 1.0, BIG, A.add, A.mult, ["pf"], ["pf4"])
-    ts(col(5), col(0), -15.0, STEP, A.add, A.mult, ["pf"], ["pf5"])
+    cp(T.ofu[:, 0:8], T.pi[:, 8:16], ["ofi"], ["ofu"])
+    ts(T.pi[:, 2:3], T.pi[:, 0:1], 12, None, A.bitwise_and, None, ["pi"], ["pj1"])
     ts(col(6), col(0), -15.0, STEP - 1.0, A.add, A.mult, ["pf"], ["pf6"])
-
-    def zero_flags(l, how):
-        a = 0
-        for u, (w, s) in enumerate(_tiles(C >> l)):
-            lo = 0 if len(s) < 4 else 16 * s[-1]
-            how(T["fl%d" % l][:, 4 * (a + lo):4 * (a + w)], 4 * (w - lo), four("fl%d.%d" % (l, u)))
-            a += w
-
-    zero_flags(0, lambda ap, n, w: fill(ap, 0.0, w))
-    zero(T.rk[:], 64, ["rk0", "rk1"])
-    zero(T.lt0[:, 448:512], 64, four("lt0.0"))
-    zero(T.lt0[:, 960:1024], 64, four("lt0.1"))
-    zero_flags(1, zero)
-    zero(T.oo1[:, 224:256], 32, ["oo1"])
-    zero(T.lt1[:, 256:512], 256, four("lt1.0"))
-    zero(T.lt1[:, 768:1024], 256, four("lt1.1"))
-    zero(T.a2t[:, 224:256], 32, four("a2o"))
-    zero(T.a2t[:, 480:512], 32, four("a2e"))
-    zero(T.u1t[:, 448:512], 64, four("u1o"))
-    zero(T.u1t[:, 960:1024], 64, four("u1e"))
-    for k in (1, 2):
-        zero(T.et[:, 520 * k + 512:520 * k + 516], 4, ["et%d" % k])
-        op("G", lambda: g.affine_select(T.et[:, 520 * k:520 * k + 512], T.et[:, 0:512], [[0, 4], [1, 2], [0, 64]], A.is_equal, 0.0, 1 - k, 0),
-           ["et0"], ["et%d" % k])
-
-    mz, kr, kk, k2, k3 = [lambda n, k=k, a=0: T.kk[:, C * k + a:C * k + n] for k in range(5)]
-    act(mz(C), T.jm[:], F.Abs, ["jm", "pf3"], ["mz"], scale=BIG, bias=col(3))
-    act(kr(C), T.jm[:], F.Relu, ["jm", "pf4"], ["kr"], scale=-BIG, bias=col(4))
-    quant("ua_", 0, 128, T.uat[:], ["uat"], ["ua_"])
-    pick("pa", 0, "ua_", 0, 128, T.ofu[:, 0:8], 128, ["ua_", "ofu"], "pa")
-    act(kk(C), kr(C), F.Copy, ["kr"], ["kk"], scale=-1.0)
-    act(k3(C), T.jm[:], F.Sign, ["jm"], ["k3"])
-    act(k2(C), kr(C), F.Identity, ["kr"], ["k2"], scale=-1.0, bias=STEP)
-
-    def units(kind, bs):
-        for b in bs:
-            quant("e_", 128 * (4 * kind + b), 128, T.et[:, 520 * kind + 3 - b:520 * kind + 515 - b], ["et%d" % kind], ["e%d.%d" % (kind, b)])
-
+    ts(col(9), T.pi[:, 2:3], STEP - 1.0, col(0), A.mult, A.add, ["pj1", "pf"], ["pf9"])
+    fill(T.rs[:], 0.0, ["rs"])
+    ts(col(7), T.pi[:, 2:3], 4.0, BIG / 4, A.add, A.mult, ["pj1"], ["pf7"])
+    fill(ends(0), LOW, ["sc0"])
     units(0, (2, 3))
-    quant("a0", 0, H, T.xt[:, 0:4 * H], ["xt0"], ["a0.0"])
-    quant("a0", H, H, T.xt[:, 4 * H:4 * C], ["xt1"], ["a0.1"])
+    op("G", lambda: g.affine_select(T.et[:, 520:1036], T.et[:, 0:516], [[1, 516]], A.not_equal, -1.0, -3, -4), ["et0"], ["et1"])
+    zero(T.lt0[:, 448:512], 64, ["lt0.0"])
+    zero(T.lt0[:, 960:1024], 64, ["lt0.1"])
+    zero_flags(1, range(4), zero)
+    iota(ends(1), [[0, 14]], int(LOW), 0, ["sc1"])
+    zero(T.lt1[:, 224:512], 288, ["lt1.0"])
+    zero(T.lt1[:, 736:1024], 288, ["lt1.1"])
+    zero(T.a2t[:, 0:64], 64, four("a2e"))
+    zero(T.a2t[:, 288:512], 224, four("a2e"))
+    zero(T.a2t[:, 736:1024], 288, four("a2o"))
+    zero(T.u1t[:, 448:512], 64, ["u1o"])
+    zero(T.u1t[:, 960:1024], 64, ["u1e"])
+    zero(T.ht1[:, 0:64], 64, ["ht1"])
 
-    def orders(l, st, atok, bv, bs, bc, bd):
+    mz, kr, kk, k3, k2 = [lambda n, k=k, a=0: T.kk[:, H * k + a:H * k + n] for k in range(5)]
+    act(mz(H), T.jm[:], F.Abs, ["jm", "pf3"], ["mz"], scale=BIG, bias=col(3))
+    act(kr(H), T.jm[:], F.Relu, ["jm", "pf4"], ["kr"], scale=-BIG, bias=col(4))
+    quant("ua_", 0, 128, T.uat[:], ["uat"], ["ua_"])
+    act(kk(H), kr(H), F.Copy, ["kr"], ["kk"], scale=-1.0)
+    pick("pa", 0, "ua_", 0, 128, T.ofu[:, 0:8], 128, ["ua_", "ofu"], "pa")
+    act(k3(H), T.jm[:], F.Sign, ["jm"], ["k3"])
+    zero_flags(0, (1, 5, 6), wipe)
+    act(T.ct[:, 32:60], T.ct[:, 0:28], F.Identity, ["ct", "pf6"], ["cst"], bias=col(6))
+    act(col(8), col(9), F.Identity, ["pf9"], ["pf8"], bias=-12 * STEP)
+    act(k2(H), kr(H), F.Identity, ["kr"], ["k2"], scale=-1.0, bias=STEP)
+    act(k2(C, a=H), kr(H), F.Identity, ["kr"], ["k2b"], scale=-1.0, bias=STEP)
+
+    def places(l):
+        n = C >> l
+        act(T["pr%d" % l][:], T.jj[:, 0:n].indirect(T.ru[:, 32 * l:32 * l + n // 16]), F.Copy, ["ru%d" % l, "jj"], ["pr%d" % l])
+
+    def orders(l, st, bv, bs, bx, bd):
         n, L = C >> l, str(l)
         nt, a_, z = n // 16, "a" + L, 32 * l
-        fl, rs = T["fl" + L], T.rs
-        mm(bv, st, 0, a_, 0, n, True, True, atok + [st + "q", st + "s"])
-        mm(bs, st, 0, a_, 0, n, True, True, atok + [st + "q", st + "s"])
-        units(l, (0, 1))
-        pv, psn = "ps%d" % bv, "ps%d" % bs
-        cut = 16 * (NV[l] + 1)
-        for lo, hi, tok in ((cut, n, "b"), (0, cut, "a")):
-            tt(T.ms[:, lo:hi], bank(bv, lo, hi), mz(hi, a=lo), A.subtract, [pv, "mz"], ["ms" + tok])
-            scan(T.cf[:, lo:hi], kk(hi, a=lo), T.ms[:, lo:hi], A.add, A.max, ["kk", "ms" + tok], ["cf" + tok])
+        fl, rs, rk, sc = T["fl" + L], T.rs, T.rk[:, z:z + nt], T["sc" + L]
+        early, main, late = CFG["rows"][l]
         tiles = _tiles(n)
         where, start, a = {}, [], 0
         for u, (w, s) in enumerate(tiles):
@@ -273,111 +293,138 @@ def rank_program(g, core, T, topo):
             for k, t in enumerate(s):
                 where[t] = (u, k)
             a += w
+        stat = [st + "q", st + "s"]
+        atok = ["a0.0", "a0.1"] if l == 0 else ["a1"]
+        cut = H if l == 0 else 16 * (main[0] + 1)
 
-        def slot(t, w):
+        def cft(t):
+            return "cfb" if 16 * t >= cut else "cfa"
+
+        def slot(t, lo, hi):
             u, k = where[t]
-            return fl[:, 4 * start[u] + k:4 * (start[u] + w):4], "fl%d.%d.%d" % (l, u, k)
+            return fl[:, 4 * (start[u] + lo) + k:4 * (start[u] + hi):4]
 
-        def close(u):
-            w = tiles[u][0]
-            quant("fl" + L, start[u], w, fl[:, 4 * start[u]:4 * (start[u] + w)], four("fl%d.%d" % (l, u)), ["flq%d.%d" % (l, u)])
-        long_ = list(range(nt - 1, NV[l], -1))
-        for i in range(len(long_) + 1):
-            if i < len(long_):
-                t = long_[i]
-                act(T.tmp[:, C * (i % 4):C * (i % 4) + 16 * t], bank(bs, 0, 16 * t), F.Sign, [psn, "cfb"], ["tmp%d" % (i % 4)],
-                    bias=T.cf[:, 16 * t + 15:16 * t + 16], scale=-1.0)
-            if i > 0:
-                t = long_[i - 1]
-                o, tok = slot(t, 16 * t)
-                act(o, T.tmp[:, C * ((i - 1) % 4):C * ((i - 1) % 4) + 16 * t], F.Relu, ["tmp%d" % ((i - 1) % 4), "rs"],
-                    [tok, "rs%d.%d" % (l, t)], accum_out=rs[:, z + t:z + t + 1])
-        o, tok = slot("d", n)
-        tt(o, bank(bv, 0, n), T.cf[:, 0:n], A.is_le, [pv, "cfa", "cfb"], [tok])
-        short = list(range(NV[l], 0, -1))
-        ns = min(NV[l], 16)
-        mine = [u for u, (w, s) in enumerate(tiles) if all(t != "d" and t <= NV[l] for t in s)]
-        theirs = [u for u in range(len(tiles)) if u not in mine]
-        work = sum(16 * t * 1.5 + 120 for t in short) + sum(tiles[u][0] + 20 for u in mine)
-        swork = sum(32 * t + 160 for t in long_)
-        due = {u: sum(32 * t + 160 for t in long_ if t >= min(x for x in tiles[u][1] if x != "d")) / swork for u in theirs}
-        done, closed = 0.0, []
-        for b in range(4):
-            mm(bd + b, "e_", 128 * b, a_, 0, n, True, True, atok + ["e0.%d" % b])
-        for i in range(len(short) + 1):
-            if i < len(short):
-                t = short[i]
-                o, tok = slot(t, 16 * t)
-                ts(o, bank(bv, 0, 16 * t), T.cf[:, 16 * t + 15:16 * t + 16], None, A.is_lt, None, [pv, "cfa"], [tok])
-            if i == 0:
-                o, tok = slot("d", n)
-                scan(T.dsc[:, 0:n], k3(n), o, A.mult, A.add, ["k3", tok], ["dsc"])
-            else:
-                t = short[i - 1]
-                o, tok = slot(t, 16 * t)
-                if t > ns:
-                    op("V", lambda: V.tensor_reduce(rs[:, z + t:z + t + 1], o, AxisListType.X, A.add), [tok, "rs"], ["rs%d.%d" % (l, t)])
-                else:
-                    scan(T.sc[:, 256 * t - 16 * t:256 * t], o, o, A.add, A.max, [tok], ["sc%d" % t])
-                if l == 0 and i == 2:
-                    quant("g_", 0, 128, T.gt[:], ["gt"], ["g_"])
-                    ts(T.ct[:, 32:60], T.ct[:, 0:28], col(6), None, A.add, None, ["ct", "pf6"], ["cst"])
-                done += 16 * t * 1.5 + 120
-                u, k = where[t]
-                if u in mine and t == tiles[u][1][-1]:
-                    close(u)
-                    closed.append(u)
-                    done += tiles[u][0] + 20
-                for u in theirs[:-1]:
-                    if u not in closed and done / work >= due[u] and all(x == "d" or x > NV[l] or x >= t for x in tiles[u][1]):
-                        close(u)
-                        closed.append(u)
-        cp(rs[:, z + 1:z + ns + 1], T.sc[:, 255:256 * ns:256], ["sc%d" % t for t in range(1, ns + 1)] + ["rs"], ["rs%d.v" % l])
-        tt(T.fi[:, 0:nt], T.ct[:, 32:32 + nt], T.dsc[:, 15:n:16], A.subtract, ["cst", "dsc"], ["fi0"])
-        for u in theirs:
-            if u not in closed:
-                close(u)
-                closed.append(u)
-        seq = [0] + [u for u in closed if u != 0]
-        for i, u in enumerate(seq):
-            mm(bc, "g_", 0, "fl" + L, start[u], tiles[u][0], i == 0, i == len(seq) - 1, ["g_", "flq%d.%d" % (l, u)])
-        for b in range(4):
-            scaled("S", T["dh" + L][:, n * b:n * b + n], bank(bd + b, 0, n), 0.5, ["ps%d" % (bd + b)], ["dh%d.%d" % (l, b)])
-        tt(T.fi[:, 64:64 + nt], T.fi[:, 0:nt], rs[:, z:z + nt], A.subtract, ["fi0", "rs%d.v" % l] + ["rs%d.%d" % (l, t) for t in range(ns + 1, nt)], ["fi1"])
+        def stok(t):
+            return "fl%d.%d.%d" % ((l,) + where[t])
+
+        def own(b, lo, hi, tok, between=None):
+            tt(T.ms[:, lo:hi], bank(b, lo, hi), mz(hi - lo), A.subtract, ["ps%d" % b, "mz"], ["ms" + tok])
+            if between:
+                between()
+            scan(T.cf[:, lo:hi], kk(hi - lo), T.ms[:, lo:hi], A.add, A.max, ["kk", "ms" + tok], ["cf" + tok])
+
+        def inside(b, lo, hi, r, tok):
+            tt(slot("d", lo, hi), bank(b, lo, hi), T.cf[:, lo:hi], A.is_le, ["ps%d" % b] + r, [tok])
+
+        def inside_sum(lo, hi, tok):
+            scan(T.dsc[:, lo:hi], k3(hi - lo), slot("d", lo, hi), A.mult, A.add, ["k3", tok], ["dsc%d" % (lo // H)])
+
+        turn = [0]
+
+        def srows(b, rows):
+            for i in range(len(rows) + 1):
+                if i < len(rows):
+                    t, k = rows[i], (turn[0] + i) % 4
+                    act(T.tmp[:, C * k:C * k + 16 * t], bank(b, 0, 16 * t), F.Sign, ["ps%d" % b, cft(t)], ["tmp%d" % k],
+                        bias=T.cf[:, 16 * t + 15:16 * t + 16], scale=-1.0)
+                if i > 0:
+                    t, k = rows[i - 1], (turn[0] + i - 1) % 4
+                    act(slot(t, 0, 16 * t), T.tmp[:, C * k:C * k + 16 * t], F.Relu, ["tmp%d" % k, "rs"],
+                        [stok(t), "rs%d.%d" % (l, t)], accum_out=rs[:, z + t:z + t + 1])
+            turn[0] += len(rows)
+
         if l == 0:
-            quant("ub_", 0, 128, T.ubt[:], ["ubt"], ["ub_"])
+            quant("a0", 0, H, T.xt[:, 0:4 * H], ["xt0"], ["a0.0"])
+            mm(bd[2], st, 0, a_, 0, H, True, True, ["a0.0"] + stat)
+            mm(bd[3], st, 0, a_, 0, H, True, True, ["a0.0"] + stat)
+            units(0, (0, 1))
+            own(bd[2], 0, H, "a")
+            srows(bd[3], early)
+            quant("a0", H, H, T.xt[:, 4 * H:4 * C], ["xt1"], ["a0.1"])
+            mm(bv, st, 0, a_, 0, n, True, True, atok + stat)
+            mm(bs, st, 0, a_, 0, n, True, True, atok + stat)
+            inside(bd[2], 0, H, ["cfa"], "fl0.0.0")
+            quant("g_", 0, 128, T.gt[:], ["gt"], ["g_"])
+            own(bv, H, n, "b", lambda: inside_sum(0, H, "fl0.0.0"))
+            dl, dtok = H, "fl0.0.4"
         else:
+            mm(bv, st, 0, a_, 0, n, True, True, atok + stat)
+            mm(bs, st, 0, a_, 0, n, True, True, atok + stat)
             units(1, (2,))
-            negate(0)
-        scan(T.csc[:, 0:n], k2(n), bank(bc, 0, n), A.add, A.max, ["k2", "ps%d" % bc], ["csc"])
-        tt(T.rk[:, z:z + nt], T.fi[:, 64:64 + nt], T.csc[:, 15:n:16], A.add, ["fi1", "csc"], ["rk" + L])
-        cp(T.ru[:, z:z + nt], T.rk[:, z:z + nt], ["rk" + L], ["ru" + L])
+            own(bv, 0, cut, "a")
+            own(bv, cut, n, "b")
+            dl, dtok = 0, "fl1.0.0"
+        for b in range(4):
+            mm(bd[b], "e_", 128 * b, a_, 0, n, True, True, atok + ["e0.%d" % b])
+        srows(bs, main + late)
+        if l == 0:
+            act(T.jq[:, H:2 * H], T.jq[:, 0:H], F.Relu, ["jq", "pf7"], ["kq"], scale=-BIG, bias=col(7))
+        for b in range(4):
+            scaled("S", T["dh" + L][:, b:4 * n:4], bank(bd[b], 0, n), 0.5, ["ps%d" % bd[b]], ["dh%d.%d" % (l, b)])
+            if l == 0 and b == 0:
+                act(T.jq[:, 2 * H:3 * H], T.jq[:, H:2 * H], F.Identity, ["kq"], ["k4"], scale=-1.0, bias=STEP)
+        if l == 1:
+            places(0)
+        plan = [(w[0], int(w[1:] or 0)) for w in CFG["plan"][l].split()]
+        rows = [t for k, t in plan if k == "c"]
+        shut, held = [u for k, u in plan if k == "q"], []
+        turns = [0] + [u for u in shut if u != 0]
+        pv = "ps%d" % bv
+        for k, t in plan:
+            if k == "d":
+                inside(bv, dl, n, ["cfa", "cfb"], dtok)
+            elif k == "e":
+                inside_sum(dl, n, dtok)
+            elif k == "c":
+                ts(slot(t, 0, 16 * t), bank(bv, 0, 16 * t), T.cf[:, 16 * t + 15:16 * t + 16], None, A.is_lt, None, [pv, cft(t)], [stok(t)])
+            elif k == "s":
+                e = n // 2 * (t + 1)
+                scan(sc[:, e - 8 * t:e], slot(t, 0, 8 * t), slot(t, 8 * t, 16 * t), A.add, A.add, [stok(t), "sc" + L], ["sc%d.%d" % (l, t)], LOW)
+            elif k == "r":
+                tt(rk, T.ct[:, 32:32 + nt], T.dsc[:, 15:n:16], A.subtract, ["cst", "dsc0", "dsc1"], ["rk" + L])
+            elif k == "a":
+                tt(rk, rk, rs[:, z:z + nt], A.subtract, ["rk" + L, "rs"] + ["rs%d.%d" % (l, t) for t in early + main + late], ["rk" + L])
+            elif k == "b":
+                tt(rk, rk, ends(l), A.subtract, ["rk" + L] + ["sc%d.%d" % (l, t) for t in rows], ["rk" + L])
+            elif k == "x":
+                scan(T.csc[:, 0:n], k2(n), bank(bx, 0, n), A.add, A.max, ["k2", "k2b", "ps%d" % bx], ["csc"])
+            elif k == "X":
+                tt(rk, rk, T.csc[:, 15:n:16], A.add, ["csc", "rk" + L], ["rk" + L])
+            else:
+                quant("fl" + L, start[t], tiles[t][0], fl[:, 4 * start[t]:4 * (start[t] + tiles[t][0])], slots(l, t), ["flq%d.%d" % (l, t)])
+                held.append(t)
+                if 0 in shut[:shut.index(t) + 1]:
+                    for v in [v for v in turns if v in held]:
+                        held.remove(v)
+                        mm(bx, "g_", 0, "fl" + L, start[v], tiles[v][0], v == 0, v == turns[-1], ["g_", "flq%d.%d" % (l, v)])
+        cp(T.ru[:, z:z + nt], rk, ["rk" + L], ["ru" + L])
         cp(T["oo" + L][:, 0:n].indirect(T.ru[:, z:z + nt]), T.jj[:, 0:n], ["ru" + L, "jj"], ["oo" + L])
-        lists(l, 0)
+        if l == 1:
+            places(1)
+        lists(l, 1)
         dma("Y", T.ol[0:8, l * C:l * C + n], T["oo" + L][0:128:16, 0:n], ["oo" + L], [])
 
-    def lists(l, half):
-        L, m = str(l), M[l]
-        for k in (2 * half + 1, 2 * half):
-            scan(T["lsc" + L][:, m * k:m * k + m], k2(m), T["oo" + L][:, (k + 2) % 4:4 * m:4], A.add, A.max, ["k2", "oo" + L], ["lsc%d.%d" % (l, k)])
-            ts(T["lu" + L][:, 8 * k:8 * k + m // 16], T["lsc" + L][:, m * k + 15:m * k + m:16], col(5), None, A.add, None,
-               ["lsc%d.%d" % (l, k), "pf5"], ["lu%d.%d" % (l, k)])
+    def aslist(out, tmp, a, row, m, r, tok):
+        scan(T[tmp][:, a:a + m], T.jq[:, 2 * H:2 * H + m], row, A.add, A.max, ["k4"] + r, [tok + "s"])
+        ts(T[out][:, a // 4:(a + m) // 4], T[tmp][:, a + 3:a + m:4], 4.0, col(8), A.mult, A.add, [tok + "s", "pf8"], [tok])
 
-    def member(l, k):
-        return T["lu%d" % l][:, 8 * k:8 * k + M[l] // 16]
+    def lists(l, odd):
+        n, L = C >> l, str(l)
+        for k in (1, 0):
+            aslist("lu" + L, "lsc" + L, n // 4 * (2 * k + odd), T["oo" + L][:, 2 * odd + k:n:4], n // 4, ["oo" + L], "lu%d.%d.%d" % (l, k, odd))
 
-    def lows(l, half):
-        n, L, m = C >> l, str(l), M[l]
-        name = "lt%d.%d" % (l, half)
-        for b in range(4):
-            a = m * (4 * half + b)
-            act(T["x1" + L][:, a:a + m], T["dh" + L][:, n * b:n * b + n].indirect(member(l, 2 * half + 1)), F.Copy,
-                ["lu%d.%d" % (l, 2 * half + 1), "dh%d.%d" % (l, b)], ["x1%d.%d.%d" % (l, half, b)])
-        for b in range(4):
-            a = m * (4 * half + b)
-            tt(T["lt" + L][:, 512 * half + b:512 * half + 4 * m:4], T["dh" + L][:, n * b:n * b + n].indirect(member(l, 2 * half)), T["x1" + L][:, a:a + m], A.add,
-               ["lu%d.%d" % (l, 2 * half), "dh%d.%d" % (l, b), "x1%d.%d.%d" % (l, half, b)], ["%s.%d" % (name, b)])
-        quant(("lo", "lw")[half] + L, 0, 128, T["lt" + L][:, 512 * half:512 * half + 512], four(name), [("lo", "lw")[half] + L])
+    def lows(l, odd):
+        n, L = C >> l, str(l)
+        c, cuts, dh = n // 16, CFG["lows"][l], T["dh" + L][:, 0:4 * n]
+        pieces = list(zip(cuts, cuts[1:]))
+        for a, z in pieces:
+            act(T["x1" + L][:, n * odd + 16 * a:n * odd + 16 * z], dh.indirect(T["lu" + L][:, c * (2 + odd) + a:c * (2 + odd) + z]), F.Copy,
+                ["lu%d.1.%d" % (l, odd)] + four("dh" + L), ["x1%d.%d.%d" % (l, odd, a)])
+        o = 512 * (1 - odd)
+        for a, z in pieces:
+            tt(T["lt" + L][:, o + 16 * a:o + 16 * z], dh.indirect(T["lu" + L][:, c * odd + a:c * odd + z]), T["x1" + L][:, n * odd + 16 * a:n * odd + 16 * z], A.add,
+               ["lu%d.0.%d" % (l, odd), "x1%d.%d.%d" % (l, odd, a), "lt%d.%d" % (l, 1 - odd)] + four("dh" + L), ["lt%d.%d.%d" % (l, odd, a)])
+        quant(("lw", "lo")[odd] + L, 0, 128, T["lt" + L][:, o:o + 512], ["lt%d.%d.%d" % (l, odd, a) for a, z in pieces], [("lw", "lo")[odd] + L])
 
     def layer(l, odd, b0, out, tok, by):
         h = (C >> l) // 4
@@ -389,104 +436,116 @@ def rank_program(g, core, T, topo):
         for b in range(4):
             scaled(by[b], out(b), bank(b0 + b, lo, lo + h), 0.03125, ["ps%d" % (b0 + b)], ["%s.%d" % (tok, b)])
 
-    def highs(l):
-        n, L, m = C >> l, str(l), M[l]
-        for half in range(2):
-            for b in range(4):
-                a, z = m * (4 * half + b), 4 * m * b
-                tt(T["hw" + L][:, z + 2 - 2 * half:z + 4 * m:4], T["dh" + L][:, n * b:n * b + n].indirect(member(l, 2 * half)), T["x1" + L][:, a:a + m], A.subtract,
-                   ["lu%d.%d" % (l, 2 * half), "dh%d.%d" % (l, b), "x1%d.%d.%d" % (l, half, b)], ["hw%d.%d.%d" % (l, half, b)])
+    made = ([], [])
 
-    def negate(l):
-        m, hw = M[l], T["hw%d" % l]
-        scaled("S", hw[:, 1:16 * m:2], hw[:, 0:16 * m:2], -1.0, four("hw%d.0" % l) + four("hw%d.1" % l), ["hn%d" % l])
+    def highs(l, a, z):
+        n, L, o = C >> l, str(l), 4 * HA[l]
+        made[l].append("ht%d.%d" % (l, a))
+        tt(T["ht" + L][:, o + 16 * a:o + 16 * z], T["dh" + L][:, 0:4 * n].indirect(T["lu" + L][:, a:z]), T["x1" + L][:, 16 * a:16 * z], A.subtract,
+           ["lu%d.0.0" % l, "lu%d.0.1" % l, "ht" + L] + four("dh" + L) + ["x1%d.%d.%d" % (l, k, c) for k in range(2) for c in CFG["lows"][l][:-1]],
+           made[l][-1:])
 
-    def state_lists():
-        ii, fi, tr = T.ii, T.fi, T.tr
-        cp(ii[:, 0:64], T.rk[:], ["rk0", "rk1"], ["ii0"])
-        ts(T.ofu[:, 8:16], T.pi[:, 16:24], col(0), None, A.add, None, ["dbi", "pf"], ["dbu"])
-        ts(ii[:, 128:192], ii[:, 0:64], 2, None, A.bitwise_and, None, ["ii0"], ["ii2"])
-        ts(ii[:, 64:128], ii[:, 0:64], 2, None, A.arith_shift_right, None, ["ii0"], ["ii1"])
-        ts(fi[:, 0:64], ii[:, 128:192], 64.0, None, A.mult, None, ["ii2"], ["fi0"])
-        tt(tr[:, 0:64], fi[:, 0:64], ii[:, 64:128], A.add, ["fi0", "ii1"], ["tr1"])
-        op("V", lambda: V.transpose(tr[:, 64:128], tr[:, 0:64]), ["tr1"], ["tr2"])
-        cp(tr[:, 128:256], tr[:, 64:128].indirect(T.ofu[:, 8:16]), ["tr2", "dbu"], ["tr3"])
-        op("V", lambda: V.transpose(tr[:, 256:384], tr[:, 128:256]), ["tr3"], ["tr4"])
-        cp(T.au[:], tr[:, 256:384], ["tr4"], ["au"])
+    def pack_highs(l):
+        quant("h%d" % l, 0, HW[l], T["ht%d" % l][:], made[l], ["h%d" % l])
 
-    def signed_highs(l, a, w):
-        L, m = str(l), M[l]
-        for b in range(4):
-            act(T["ht" + L][:, 4 * a + b:4 * (a + w):4], T["hw" + L][:, 4 * m * b:4 * m * (b + 1)].indirect(T.ru[:, 32 * l + a // 16:32 * l + (a + w) // 16]),
-                F.Copy, ["ru" + L, "hn" + L], ["ht%d.%d.%d" % (l, a, b)])
+    def unpack_highs(l, b0):
+        w = HW[l]
+        for b in range(2):
+            mm(b0 + b, "e_", 128 * b, "h%d" % l, 0, w, True, True, ["h%d" % l, "e0.%d" % b])
+        for b in range(2):
+            scaled("S", T["hd%d" % l][:, w * b:w * b + w], bank(b0 + b, 0, w), 1.0, ["ps%d" % (b0 + b)], ["hd%d.%d" % (l, b)])
 
-    def lay_highs(l, b0, a, w):
-        quant("h%d" % l, a, w, T["ht%d" % l][:, 4 * a:4 * (a + w)], four("ht%d.%d" % (l, a)), ["h%d.%d" % (l, a)])
-        for b in range(4):
-            mm(b0 + b, "e_", 128 * b, "h%d" % l, a, w, True, False, ["h%d.%d" % (l, a), "e0.%d" % b])
+    def lay(l, odd, banks):
+        for i, k in enumerate(banks):
+            b, s = 2 + i // 2, i % 2
+            mm(k, "e_", 128 * (2 * s + b), "h%d" % l, (HW[l] - 128) * odd, 128, True, False, ["h%d" % l, "e%d.%d" % (s, b)])
 
-    def put_back(l, b0, a, w, src, lo, hi, r):
-        for k, name in enumerate(("pe", "po")):
-            o = 64 * l + 32 * k
-            pick("%s%d" % (name, l), a, src, lo, hi, T.au[:, o + a // 16:o + (a + w) // 16], w, r + ["au"], "%s%d.%d" % (name, l, a))
-        for k, name in enumerate(("pe", "po")):
-            for b in range(4):
-                mm(b0 + b, "e_", 128 * (4 + 4 * k + b), "%s%d" % (name, l), a, w, False, k == 1,
-                   ["%s%d.%dq" % (name, l, a), "%s%d.%ds" % (name, l, a), "e%d.%d" % (k + 1, b)])
+    def rise(l, odd, src, r, vb, sb_):
+        n = C >> l
+        h = n // 4
+        lo = 128 - h if odd else HA[l]
+        for k, b, first in ((sb_[0], 2, 0), (vb[0], 0, 1), (sb_[1], 2, 0), (sb_[2], 3, 0), (vb[1], 1, 1), (sb_[3], 3, 0)):
+            mm(k, "e_", 128 * b, src, h if odd else 0, 128, first == 1, True, r + ["e0.%d" % b])
+        for i in range(4):
+            b, s = i // 2, i % 2
+            a, o = HW[l] * b + HA[l] + h * odd, 4 * (2 * odd + s) + b
+            tt(T["wn%d" % l][:, o:4 * n:16], bank(vb[b], lo, lo + h), T["hd%d" % l][:, a:a + h], (A.add, A.subtract)[s],
+               ["ps%d" % vb[b], "hd%d.%d" % (l, b)], ["wn%d.%d" % (l, o)])
+            scaled("S", T["wn%d" % l][:, o + 2:4 * n:16], bank(sb_[i], lo, lo + h), 1.0, ["ps%d" % sb_[i]], ["wn%d.%d" % (l, o + 2)])
 
-    parts = ((0, CUT), (CUT, C - CUT))
-    orders(0, "pa", ["a0.0", "a0.1"], 0, 1, 2, 4)
-    lows(0, 0)
-    swap(0, 0, "lo0", "lw0", 128, 112, ["lo0"], ["land0"])
-    lists(0, 1)
+    def fetch(l, out, o, a, w, v, r, tok):
+        n = C >> l
+        for e, lo, hi in (("V", 0, v), ("S", v, w)):
+            scaled(e, T[out][:, 4 * (o + lo):4 * (o + hi)], T["wn%d" % l][:, 0:4 * n].indirect(T["pu%d" % l][:, (a + lo) // 4:(a + hi) // 4]), 1.0,
+                   ["wn%d.%d" % (l, k) for k in range(16)] + r, [tok + e])
+
+    hc = CFG["highs"]
+    orders(0, "pa", 0, 1, 2, (6, 7, 4, 5))
     lows(0, 1)
+    swap(0, 0, "lo0", "lw0", 128, 112, ["lo0"], ["land0"])
+    lists(0, 0)
+    lows(0, 0)
+    quant("ub_", 0, 128, T.ubt[:], ["ubt"], ["ub_"])
     layer(0, False, 4, lambda b: T.a1t[:, b:4 * H:8], "a1e", "SSSS")
     pick("pb", 0, "ub_", 0, 128, T.ofu[:, 0:8], 128, ["ub_", "ofu"], "pb")
-    highs(0)
-    layer(0, True, 0, lambda b: T.a1t[:, 4 + b:4 * H:8], "a1o", "SSSV")
+    highs(0, hc[0], hc[1])
+    layer(0, True, 0, lambda b: T.a1t[:, 4 + b:4 * H:8], "a1o", "SVSV")
     quant("a1", 0, H, T.a1t[:], four("a1e") + four("a1o"), ["a1"])
-    orders(1, "pb", ["a1"], 4, 5, 6, 0)
-    lows(1, 0)
-    swap(1, 1, "lo1", "lw1", 128, 56, ["lo1"], ["land1"])
-    lists(1, 1)
+    orders(1, "pb", 4, 5, 6, (0, 1, 2, 3))
     lows(1, 1)
-    layer(1, False, 4, lambda b: T.a2t[:, 256 + b:256 + 224:4], "a2e", "SSSS")
-    highs(1)
-    negate(1)
-    signed_highs(1, 0, H)
-    layer(1, True, 0, lambda b: T.a2t[:, b:224:4], "a2o", "VVVV")
-    quant("a2", 0, 128, T.a2t[:], four("a2e") + four("a2o"), ["a2"])
-    swap(2, 1, "a2", "a2", 192, 56, ["a2"], ["land2"])
-    state_lists()
-    lay_highs(1, 4, 0, H)
-    signed_highs(0, *parts[1])
+    swap(1, 1, "lo1", "lw1", 128, 56, ["lo1"], ["land1"])
+    lists(1, 0)
+    lows(1, 0)
+    layer(1, False, 4, lambda b: T.a2t[:, 64 + b:288:4], "a2e", "SSSS")
+    highs(1, 0, 28)
     units(1, (3,))
-    units(2, range(4))
-    put_back(1, 4, 0, H, "a2", 64, 256, ["a2", "land2"])
+    highs(0, hc[1], hc[2])
+    layer(1, True, 0, lambda b: T.a2t[:, 512 + b:512 + 224:4], "a2o", "SVSV")
+    quant("a2o", 0, 128, T.a2t[:, 512:1024], four("a2o"), ["a2o"])
+    swap(2, 1, "a2o", "a2", 128, 56, ["a2o"], ["land2"])
+    pack_highs(1)
+    quant("a2", 0, 128, T.a2t[:, 0:512], four("a2e"), ["a2"])
+    unpack_highs(1, 0)
+    lay(1, 0, (4, 5, 6, 7))
+    for k in range(2):
+        aslist("pu1", "psc1", 112 * k, T.pr1[:, 1 - k:H:2], 112, ["pr1"], "pu1.%d" % k)
+    rise(1, 0, "a2", ["a2"], (2, 3), (4, 5, 6, 7))
+    lay(1, 1, (4, 5, 6, 7))
+    highs(0, hc[2], hc[3])
+    aslist("pu0", "psc0", H, T.pr0[:, H:C], H, ["pr0"], "pu0.1")
+    pack_highs(0)
+    rise(1, 1, "a2", ["a2", "land2"], (2, 3), (4, 5, 6, 7))
+    fetch(1, "u1t", 0, 0, 112, 56, ["pu1.0", "u1o"], "u1o")
+    quant("u1o", 0, 128, T.u1t[:, 0:512], ["u1oV", "u1oS"], ["u1oq"])
+    swap(3, 0, "u1o", "u1", 128, 112, ["u1oq"], ["land3"])
+    lay(0, 0, (4, 5, 6, 7))
+    fetch(1, "u1t", 128, 112, 112, 56, ["pu1.1", "u1e"], "u1e")
+    unpack_highs(0, 0)
+    quant("u1", 0, 128, T.u1t[:, 512:1024], ["u1eV", "u1eS"], ["u1"])
+    aslist("pu0", "psc0", 0, T.pr0[:, 0:H], H, ["pr0"], "pu0.0")
+    rise(0, 0, "u1", ["u1"], (2, 3), (4, 5, 6, 7))
+    lay(0, 1, (0, 1, 4, 5))
     quant("v_", 0, 128, T.vt[:], ["vt"], ["v_"])
-    for b in range(4):
-        scaled("VS"[b % 2], T.u1t[:, b:448:4], bank(4 + b, 1, H, 2), 1.0, ["ps%d" % (4 + b)], ["u1o.%d" % b])
-    quant("u1o", 0, 128, T.u1t[:, 0:512], four("u1o"), ["u1o"])
-    swap(3, 0, "u1o", "u1", 128, 112, ["u1o"], ["land3"])
-    signed_highs(0, *parts[0])
-    for b in range(4):
-        scaled("V", T.u1t[:, 512 + b:512 + 448:4], bank(4 + b, 0, H, 2), 1.0, ["ps%d" % (4 + b)], ["u1e.%d" % b])
-    quant("u1", 0, 128, T.u1t[:, 512:1024], four("u1e"), ["u1"])
-    lay_highs(0, 4, *parts[1])
-    lay_highs(0, 0, *parts[0])
-    for h, (a, w) in enumerate(parts):
-        put_back(0, 4 * h, a, w, "u1", 0, 240, ["u1", "land3"])
-    for h, (a, w) in enumerate(parts):
-        for b in range(4):
-            scaled("VS"[b % 2], T.u0t[:, 4 * a + b:4 * (a + w):4], bank(4 * h + b, 0, w), 1.0, ["ps%d" % (4 * h + b)], ["u0t.%d.%d" % (h, b)])
-        quant("u0", a, w, T.u0t[:, 4 * a:4 * (a + w)], four("u0t.%d" % h), ["u0.%d" % h])
-        mm(4 * h, "v_", 0, "u0", a, w, True, True, ["v_", "u0.%d" % h])
+    rise(0, 1, "u1", ["u1", "land3"], (2, 3), (0, 1, 4, 5))
+    parts, a = [], 0
+    for w, v in CFG["parts"]:
+        parts.append((a, w, v))
+        a += w
+
+    def store(h):
+        a, w, v = parts[h]
+        scaled("S", T.yt[:, a:a + w], bank(h, 0, w), 1.0, ["ps%d" % h], ["yt%d" % h])
+        dma("S" if h == len(parts) - 1 else "Y", T.y[:, a:a + w], T.yt[:, a:a + w], ["yt%d" % h], [])
+
+    for h, (a, w, v) in enumerate(parts):
+        fetch(0, "u0t", a, a, w, v, ["pu0.0", "pu0.1"], "u0t%d" % h)
+        quant("u0", a, w, T.u0t[:, 4 * a:4 * (a + w)], ["u0t%dV" % h, "u0t%dS" % h], ["u0.%d" % h])
+        mm(h, "v_", 0, "u0", a, w, True, True, ["v_", "u0.%d" % h])
         dma("Y", T.oc[:, 4 * a:4 * (a + w)], T.u0q[:, a:a + w].bitcast(dt.uint8), ["u0.%d" % h], [])
-        if h == 1:
-            for k in range(4):
-                dma("Y", T.osc[4 * k:4 * k + 4, 0:C], T.u0s[32 * k:32 * k + 4, 0:C], ["u0.0", "u0.1"], [])
-    for h, (a, w) in enumerate(parts):
-        scaled("S", T.yt[:, a:a + w], bank(4 * h, 0, w), 1.0, ["ps%d" % (4 * h)], ["yt%d" % h])
-        dma("S", T.y[:, a:a + w], T.yt[:, a:a + w], ["yt%d" % h], [])
+        if h > 0:
+            store(h - 1)
+    for k in range(4):
+        dma("Y", T.osc[4 * k:4 * k + 4, 0:C], T.u0s[32 * k:32 * k + 4, 0:C], ["u0.%d" % h for h in range(len(parts))], [])
+    store(len(parts) - 1)
     for sem, val in total.items():
         g.wait_ge(T.sem[sem], val)

@@ -11,13 +11,29 @@ HW = (224, 128)
 HA = (0, 16)
 BF, F32, I32, U16, Q8, U8 = "bfloat16", "float32", "int32", "uint16", "float8_e4m3fn_x4", "uint8"
 CFG = {
-    "rows": (([13, 12, 11], [21, 20, 19, 18, 17], [10, 9, 8, 7, 6, 5, 4, 3, 2]), ([], [6, 5], [9, 8, 7, 4, 3, 2])),
-    "plan": ("d c27 e c26 r s27 c25 s26 c24 s25 c23 q0 s24 c22 s23 c16 s22 c15 s16 c14 s15 q1 c1 s14 q3 s1 q2 q4 q5 q6 a b x X",
-             "d c13 e c12 r s13 c11 s12 c10 s11 c1 q0 s10 s1 q1 q2 q3 b a x X"),
-    "lows": ((0, 10, 20, 28), (0, 8, 14)),
-    "highs": (0, 20, 36, 56),
-    "parts": ((224, 112), (224, 96)),
+    "rows": (([9, 10, 5, 8, 12], [11, 14, 3, 20, 13, 15, 21, 19, 6], [7, 2]), ([], [7, 6], [5, 8, 4, 2])),
+    "plan": ("c25 c27 d c23 c26 c17 s26 c24 s25 e c22 q0 c16 s22 r c4 c1 s24 s4 s1 s27 c18 q4 s18 s16 s23 s17 b q1 q2 q3 q5 q6 a x X",
+             "c3 c1 d c12 c10 s12 c9 e c11 c13 s9 s3 s1 s10 s11 s13 r b q0 q1 q2 q3 a x X"),
+    "lows": (((0, 10, 20, 28), (0, 6, 16, 28)), ((0, 8, 14), (0, 6, 14))),
+    "lowv": ((0, 1), (0, 1)),
+    "end": "c0Y c1Y s0Y y0Y s1Y s2Y s3Y y1S",
+    "yc": "VS",
 }
+ORDER = [
+    1, 0, 2, 7, 8, 9, 10, 12, 25, 26, 27, 28, 29, 30, 31, 32, 33, 34, 35, 37, 38, 39, 64, 11, 22, 57, 23, 56, 24, 49, 58, 60, 50, 63, 52, 36, 53, 48,
+    59, 51, 54, 3, 4, 77, 5, 61, 6, 62, 78, 65, 14, 17, 79, 66, 82, 72, 70, 67, 75, 68, 133, 134, 84, 80, 69, 15, 18, 19, 16, 20, 92, 73, 74, 95, 90,
+    76, 71, 121, 118, 119, 81, 117, 124, 93, 89, 21, 13, 40, 41, 45, 94, 100, 91, 97, 120, 85, 86, 87, 88, 128, 129, 139, 122, 126, 140, 44, 103, 102,
+    141, 43, 98, 96, 105, 46, 101, 136, 127, 130, 147, 135, 123, 145, 149, 148, 99, 106, 150, 104, 108, 47, 109, 175, 142, 144, 151, 125, 107, 152,
+    110, 55, 137, 83, 143, 153, 111, 155, 132, 138, 131, 42, 176, 154, 113, 156, 354, 146, 158, 179, 157, 177, 116, 200, 159, 160, 161, 112, 115, 114,
+    217, 163, 162, 165, 183, 202, 164, 182, 166, 168, 184, 167, 169, 171, 186, 170, 185, 216, 187, 172, 189, 174, 173, 190, 188, 191, 201, 195, 199,
+    192, 193, 194, 196, 197, 198, 204, 203, 205, 208, 207, 209, 206, 211, 212, 210, 213, 214, 222, 215, 294, 218, 220, 223, 219, 225, 238, 221, 224,
+    243, 242, 226, 227, 231, 228, 229, 230, 233, 234, 235, 232, 236, 237, 240, 245, 244, 250, 253, 251, 248, 246, 260, 261, 249, 262, 264, 266, 239,
+    263, 265, 241, 267, 252, 256, 257, 255, 254, 258, 247, 259, 269, 268, 270, 271, 272, 273, 316, 277, 274, 275, 285, 284, 276, 286, 278, 279, 288,
+    287, 315, 280, 281, 282, 290, 289, 181, 180, 178, 283, 291, 292, 317, 293, 298, 297, 296, 302, 299, 300, 301, 303, 306, 304, 307, 309, 310, 311,
+    312, 295, 318, 321, 322, 319, 313, 320, 308, 338, 314, 337, 305, 326, 324, 335, 323, 325, 327, 330, 328, 329, 333, 347, 334, 331, 332, 336, 341,
+    340, 342, 346, 348, 345, 339, 352, 343, 350, 349, 351, 344, 353, 355, 356, 357, 365, 359, 360, 358, 361, 362, 366, 369, 367, 363, 364, 370, 368,
+    372, 371, 381, 375, 373, 374, 376, 382, 383, 377, 378, 384, 386, 379, 380, 394, 387, 385, 388, 395, 393, 392, 389, 396, 390, 391, 397, 398, 399,
+    400, 401, 402, 403, 404, 405, 406]
 
 
 def _tiles(n):
@@ -46,7 +62,8 @@ def _scratch():
     sb("gt", 512, BF); sb("et", 2 * 520, BF); mx("g_", 128); mx("e_", 6 * 128)
     sb("ms", C, F32); sb("cf", C, F32); sb("tmp", 4 * C, BF); sb("dsc", C, BF); sb("csc", C, F32)
     sb("rk", 64, F32); sb("ru", 64, U16); sb("rs", 64, F32)
-    sb("a1t", 2 * C, BF); sb("a2t", 1024, BF); mx("a2", 184); mx("a2o", 128)
+    sb("a1t", 2 * C, BF); sb("a2t", 512, BF); mx("a2", 184)
+    sb("tab", H, F32); sb("pr1", H, F32); sb("psc1", 240, F32); sb("pu1", 16, U16)
     sb("u1t", 1024, BF); mx("u1", 240); mx("u1o", 128)
     sb("u0t", 4 * C, BF); mx("u0", C); sb("yt", C, F32)
     for l in range(2):
@@ -55,9 +72,8 @@ def _scratch():
         L = str(l)
         sb("fl" + L, 4 * w, BF); mx("fl" + L, w); sb("sc" + L, n // 2 * (n // 16), BF)
         sb("oo" + L, n, F32); sb("lsc" + L, n, F32); sb("lu" + L, n // 4, U16); sb("dh" + L, 4 * n, BF); sb("x1" + L, 2 * n, BF)
-        sb("lt" + L, 1024, BF); mx("lo" + L, 128); mx("lw" + L, 128 + n // 4)
+        sb("lt" + L, 1024, BF); mx("lo" + L, 128); mx("lw" + L, (240, 192)[l])
         sb("ht" + L, 4 * HW[l], BF); mx("h" + L, HW[l]); sb("hd" + L, 2 * HW[l], BF); sb("wn" + L, 4 * n, BF)
-        sb("pr" + L, n, F32); sb("psc" + L, n, F32); sb("pu" + L, n // 4, U16)
     s["ps"] = ("psum", [128, 4096], F32)
     return s
 
@@ -75,6 +91,7 @@ def rank_program(g, core, T, topo):
     seen = {e: {} for e in Q}
     wrote, read = {}, {}
     ndma = [0]
+    calls = []
 
     def need(e, r, w):
         want = {}
@@ -106,29 +123,35 @@ def rank_program(g, core, T, topo):
             read[t] = {}
 
     def op(e, fn, r, w):
-        need(e, r, w)
-        fn().then_inc(T.sem[e], 1)
-        total[e] = total.get(e, 0) + 1
-        mark(e, e, r, w)
+        def issue():
+            need(e, r, w)
+            fn().then_inc(T.sem[e], 1)
+            total[e] = total.get(e, 0) + 1
+            mark(e, e, r, w)
+        calls.append(issue)
 
     def dma(e, out, in_, r, w):
-        need(e, r, w)
-        sem = "d%d" % ndma[0]
-        ndma[0] += 1
-        Q[e].dma_start(out, in_).then_inc(T.sem[sem], 16)
-        total[sem] = 16
-        mark(sem, "dma", r, w)
+        def issue():
+            need(e, r, w)
+            sem = "d%d" % ndma[0]
+            ndma[0] += 1
+            Q[e].dma_start(out, in_).then_inc(T.sem[sem], 16)
+            total[sem] = 16
+            mark(sem, "dma", r, w)
+        calls.append(issue)
 
-    def swap(k, l, src, dst, b, cols, r, w):
-        peer = T.cores[rank ^ (1 << l)]
-        rid, pid = topo.addr(peer)[:2]
-        m, sem = topo.mask(core, peer), "arr%d" % k
-        need("G", r, [])
-        g.remote_dma(T[dst + "q"][:, b:b + cols].bitcast(dt.uint8), T[src + "q"][:, 0:cols].bitcast(dt.uint8), T.sem[sem], T.sem.sent, pid, rid, m)
-        g.remote_dma(T[dst + "s"][:, b:b + cols], T[src + "s"][:, 0:cols], T.sem[sem], T.sem.sent, pid, rid, m)
-        total["sent"] = total.get("sent", 0) + 2 * len(topo.engines(core, peer))
-        total[sem] = 2 * len(topo.engines(peer, core))
-        mark(sem, "far", [], w)
+    def swap(k, l, src, a, dst, b, cols, r, w):
+        def issue():
+            peer = T.cores[rank ^ (1 << l)]
+            rid, pid = topo.addr(peer)[:2]
+            m, sem = topo.mask(core, peer), "arr%d" % k
+            need("G", r, [])
+            g.remote_dma(T[dst + "q"][:, b:b + cols].bitcast(dt.uint8), T[src + "q"][:, a:a + cols].bitcast(dt.uint8), T.sem[sem], T.sem.sent, pid, rid, m)
+            g.remote_dma(T[dst + "s"][:, b:b + cols], T[src + "s"][:, a:a + cols], T.sem[sem], T.sem.sent, pid, rid, m)
+            total["sent"] = total.get("sent", 0) + 2 * len(topo.engines(core, peer))
+            total[sem] = 2 * len(topo.engines(peer, core))
+            mark(sem, "far", [], w)
+        calls.append(issue)
 
     V, S, PE = g.vector, g.scalar, g.tensor
 
@@ -177,9 +200,10 @@ def rank_program(g, core, T, topo):
         else:
             act(out, in_, F.Copy, r, w, scale=c)
 
-    def pick(dst, a, src, lo, hi, off, n, r, w):
-        cp(T[dst + "q"][:, a:a + n].bitcast(dt.uint32), T[src + "q"][:, lo:hi].bitcast(dt.uint32).indirect(off), r, [w + "q"])
-        act(T[dst + "s"][:, a:a + n], T[src + "s"][:, lo:hi].indirect(off), F.Copy, r, [w + "s"])
+    def pick(dst, src, r):
+        off = T.ofu[:, 0:8]
+        cp(T[dst + "q"][:].bitcast(dt.uint32), T[src + "q"][:].bitcast(dt.uint32).indirect(off), r + ["ofu"], [dst + "q"])
+        act(T[dst + "s"][:], T[src + "s"][:].indirect(off), F.Copy, r + ["ofu"], [dst + "s"])
 
     def iota(out, pattern, base, cm, w, small=True):
         if small:
@@ -197,12 +221,11 @@ def rank_program(g, core, T, topo):
         return four("fl%d.%d" % (l, u)) + (["fl0.0.4"] if l == 0 and u == 0 else [])
 
     def zero_flags(l, us, how):
-        a = 0
-        for u, (w, s) in enumerate(_tiles(C >> l)):
-            lo = 0 if len(s) < 4 else 16 * s[-1]
-            if u in us:
-                how(T["fl%d" % l][:, 4 * (a + lo):4 * (a + w)], 4 * (w - lo), slots(l, u))
-            a += w
+        tiles = _tiles(C >> l)
+        for u in us:
+            w, s = tiles[u]
+            a, lo = sum(t[0] for t in tiles[:u]), 0 if len(s) < 4 else 16 * s[-1]
+            how(T["fl%d" % l][:, 4 * (a + lo):4 * (a + w)], 4 * (w - lo), slots(l, u))
 
     def ends(l):
         h = C >> (l + 1)
@@ -221,6 +244,7 @@ def rank_program(g, core, T, topo):
     dma("Y", T.vt[:], T.v[:], [], ["vt"])
 
     iota(T.pi[:, 0:1], [[0, 1]], 0, 1, ["pi"], False)
+    iota(col(1), [[0, 1]], 0, 1, ["pf1"])
     iota(T.jn[:], [[1, 128]], 0, 0, ["jn"])
     iota(T.pi[:, 8:16], [[16, 8]], 0, 0, ["ofi"], False)
     iota(T.jm[:], [[0, H // 16], [1, 16]], 0, 0, ["jm"])
@@ -228,19 +252,19 @@ def rank_program(g, core, T, topo):
     iota(T.ct[:, 0:28], [[16, 28]], int(LOW), 0, ["ct"])
     op("G", lambda: g.affine_select(T.gt[:], T.one[:], [[-16, 8], [0, 64]], A.is_ge, 0.0, 0, 1), ["one"], ["gt"])
     op("G", lambda: g.affine_select(T.gt[:], T.gt[:], [[16, 8], [0, 64]], A.is_ge, 0.0, 15, -1), ["gt"], ["gt"])
+    zero_flags(0, (3, 6, 2, 1), zero)
     iota(T.jj[:], [[1, C]], 0, 0, ["jj"])
     iota(T.jq[:, 0:H], [[0, H // 4], [1, 4]], 0, 0, ["jq"])
 
     def wipe(ap, n, w):
         act(ap, T.one[:, 0:n], F.Copy, ["one"], w, scale=0.0)
 
-    zero_flags(0, (3, 4, 0, 2), wipe)
+    zero_flags(0, (4, 5, 0), wipe)
     ts(T.pi[:, 1:2], T.pi[:, 0:1], 15, None, A.bitwise_and, None, ["pi"], ["pj0"])
     fill(T.et[:, 0:516], 0.0, ["et0"])
     cp(col(0), T.pi[:, 1:2], ["pj0"], ["pf"])
-    cp(col(1), T.pi[:, 0:1], ["pi"], ["pf1"])
-    ts(col(3), col(0), -BIG, None, A.mult, None, ["pf"], ["pf3"])
     ts(T.et[:, 3:515:4], T.jn[:], col(1), None, A.is_equal, None, ["jn", "pf1"], ["et0"])
+    ts(col(3), col(0), -BIG, None, A.mult, None, ["pf"], ["pf3"])
     ts(col(4), col(0), 1.0, BIG, A.add, A.mult, ["pf"], ["pf4"])
     cp(T.ofu[:, 0:8], T.pi[:, 8:16], ["ofi"], ["ofu"])
     ts(T.pi[:, 2:3], T.pi[:, 0:1], 12, None, A.bitwise_and, None, ["pi"], ["pj1"])
@@ -250,36 +274,24 @@ def rank_program(g, core, T, topo):
     ts(col(7), T.pi[:, 2:3], 4.0, BIG / 4, A.add, A.mult, ["pj1"], ["pf7"])
     fill(ends(0), LOW, ["sc0"])
     units(0, (2, 3))
-    op("G", lambda: g.affine_select(T.et[:, 520:1036], T.et[:, 0:516], [[1, 516]], A.not_equal, -1.0, -3, -4), ["et0"], ["et1"])
     zero(T.lt0[:, 448:512], 64, ["lt0.0"])
     zero(T.lt0[:, 960:1024], 64, ["lt0.1"])
+    op("G", lambda: g.affine_select(T.et[:, 520:1036], T.et[:, 0:516], [[1, 516]], A.not_equal, -1.0, -3, -4), ["et0"], ["et1"])
     zero_flags(1, range(4), zero)
     iota(ends(1), [[0, 14]], int(LOW), 0, ["sc1"])
-    zero(T.lt1[:, 224:512], 288, ["lt1.0"])
-    zero(T.lt1[:, 736:1024], 288, ["lt1.1"])
-    zero(T.a2t[:, 0:64], 64, four("a2e"))
-    zero(T.a2t[:, 288:512], 224, four("a2e"))
-    zero(T.a2t[:, 736:1024], 288, four("a2o"))
-    zero(T.u1t[:, 448:512], 64, ["u1o"])
-    zero(T.u1t[:, 960:1024], 64, ["u1e"])
-    zero(T.ht1[:, 0:64], 64, ["ht1"])
 
     mz, kr, kk, k3, k2 = [lambda n, k=k, a=0: T.kk[:, H * k + a:H * k + n] for k in range(5)]
     act(mz(H), T.jm[:], F.Abs, ["jm", "pf3"], ["mz"], scale=BIG, bias=col(3))
     act(kr(H), T.jm[:], F.Relu, ["jm", "pf4"], ["kr"], scale=-BIG, bias=col(4))
     quant("ua_", 0, 128, T.uat[:], ["uat"], ["ua_"])
     act(kk(H), kr(H), F.Copy, ["kr"], ["kk"], scale=-1.0)
-    pick("pa", 0, "ua_", 0, 128, T.ofu[:, 0:8], 128, ["ua_", "ofu"], "pa")
+    pick("pa", "ua_", ["ua_"])
     act(k3(H), T.jm[:], F.Sign, ["jm"], ["k3"])
-    zero_flags(0, (1, 5, 6), wipe)
     act(T.ct[:, 32:60], T.ct[:, 0:28], F.Identity, ["ct", "pf6"], ["cst"], bias=col(6))
     act(col(8), col(9), F.Identity, ["pf9"], ["pf8"], bias=-12 * STEP)
+    act(col(10), col(0), F.Identity, ["pf"], ["pf10"], scale=STEP, bias=-15 * STEP)
     act(k2(H), kr(H), F.Identity, ["kr"], ["k2"], scale=-1.0, bias=STEP)
     act(k2(C, a=H), kr(H), F.Identity, ["kr"], ["k2b"], scale=-1.0, bias=STEP)
-
-    def places(l):
-        n = C >> l
-        act(T["pr%d" % l][:], T.jj[:, 0:n].indirect(T.ru[:, 32 * l:32 * l + n // 16]), F.Copy, ["ru%d" % l, "jj"], ["pr%d" % l])
 
     def orders(l, st, bv, bs, bx, bd):
         n, L = C >> l, str(l)
@@ -317,7 +329,7 @@ def rank_program(g, core, T, topo):
             tt(slot("d", lo, hi), bank(b, lo, hi), T.cf[:, lo:hi], A.is_le, ["ps%d" % b] + r, [tok])
 
         def inside_sum(lo, hi, tok):
-            scan(T.dsc[:, lo:hi], k3(hi - lo), slot("d", lo, hi), A.mult, A.add, ["k3", tok], ["dsc%d" % (lo // H)])
+            scan(T.dsc[:, lo:hi], k3(hi - lo), slot("d", lo, hi), A.mult, A.add, ["k3", tok], ["dsc%d" % (lo > 0)])
 
         turn = [0]
 
@@ -350,7 +362,7 @@ def rank_program(g, core, T, topo):
         else:
             mm(bv, st, 0, a_, 0, n, True, True, atok + stat)
             mm(bs, st, 0, a_, 0, n, True, True, atok + stat)
-            units(1, (2,))
+            units(1, (2, 3))
             own(bv, 0, cut, "a")
             own(bv, cut, n, "b")
             dl, dtok = 0, "fl1.0.0"
@@ -363,20 +375,17 @@ def rank_program(g, core, T, topo):
             scaled("S", T["dh" + L][:, b:4 * n:4], bank(bd[b], 0, n), 0.5, ["ps%d" % bd[b]], ["dh%d.%d" % (l, b)])
             if l == 0 and b == 0:
                 act(T.jq[:, 2 * H:3 * H], T.jq[:, H:2 * H], F.Identity, ["kq"], ["k4"], scale=-1.0, bias=STEP)
-        if l == 1:
-            places(0)
         plan = [(w[0], int(w[1:] or 0)) for w in CFG["plan"][l].split()]
         rows = [t for k, t in plan if k == "c"]
         shut, held = [u for k, u in plan if k == "q"], []
         turns = [0] + [u for u in shut if u != 0]
-        pv = "ps%d" % bv
         for k, t in plan:
             if k == "d":
                 inside(bv, dl, n, ["cfa", "cfb"], dtok)
             elif k == "e":
                 inside_sum(dl, n, dtok)
             elif k == "c":
-                ts(slot(t, 0, 16 * t), bank(bv, 0, 16 * t), T.cf[:, 16 * t + 15:16 * t + 16], None, A.is_lt, None, [pv, cft(t)], [stok(t)])
+                ts(slot(t, 0, 16 * t), bank(bv, 0, 16 * t), T.cf[:, 16 * t + 15:16 * t + 16], None, A.is_lt, None, ["ps%d" % bv, cft(t)], [stok(t)])
             elif k == "s":
                 e = n // 2 * (t + 1)
                 scan(sc[:, e - 8 * t:e], slot(t, 0, 8 * t), slot(t, 8 * t, 16 * t), A.add, A.add, [stok(t), "sc" + L], ["sc%d.%d" % (l, t)], LOW)
@@ -400,152 +409,154 @@ def rank_program(g, core, T, topo):
         cp(T.ru[:, z:z + nt], rk, ["rk" + L], ["ru" + L])
         cp(T["oo" + L][:, 0:n].indirect(T.ru[:, z:z + nt]), T.jj[:, 0:n], ["ru" + L, "jj"], ["oo" + L])
         if l == 1:
-            places(1)
+            act(T.pr1[:], T.tab[:].indirect(T.ru[:, z:z + nt]), F.Copy, ["ru1", "tab"], ["pr1"])
         lists(l, 1)
         dma("Y", T.ol[0:8, l * C:l * C + n], T["oo" + L][0:128:16, 0:n], ["oo" + L], [])
 
-    def aslist(out, tmp, a, row, m, r, tok):
-        scan(T[tmp][:, a:a + m], T.jq[:, 2 * H:2 * H + m], row, A.add, A.max, ["k4"] + r, [tok + "s"])
-        ts(T[out][:, a // 4:(a + m) // 4], T[tmp][:, a + 3:a + m:4], 4.0, col(8), A.mult, A.add, [tok + "s", "pf8"], [tok])
-
     def lists(l, odd):
         n, L = C >> l, str(l)
-        for k in (1, 0):
-            aslist("lu" + L, "lsc" + L, n // 4 * (2 * k + odd), T["oo" + L][:, 2 * odd + k:n:4], n // 4, ["oo" + L], "lu%d.%d.%d" % (l, k, odd))
+        a, m, tok = n // 2 * odd, n // 4, "lu%d.%d" % (l, odd)
+        for k in range(2):
+            scan(T["lsc" + L][:, a + k * m:a + k * m + m], T.jq[:, 2 * H:2 * H + m], T["oo" + L][:, 2 * odd + k:n:4], A.add, A.max,
+                 ["k4", "oo" + L], ["%s.%d" % (tok, k)])
+        ts(T["lu" + L][:, a // 4:(a + 2 * m) // 4], T["lsc" + L][:, a + 3:a + 2 * m:4], 4.0, col(8), A.mult, A.add, [tok + ".0", tok + ".1", "pf8"], [tok])
 
     def lows(l, odd):
         n, L = C >> l, str(l)
-        c, cuts, dh = n // 16, CFG["lows"][l], T["dh" + L][:, 0:4 * n]
+        c, cuts, dh = n // 16, CFG["lows"][l][odd], T["dh" + L][:, 0:4 * n]
         pieces = list(zip(cuts, cuts[1:]))
-        for a, z in pieces:
-            act(T["x1" + L][:, n * odd + 16 * a:n * odd + 16 * z], dh.indirect(T["lu" + L][:, c * (2 + odd) + a:c * (2 + odd) + z]), F.Copy,
-                ["lu%d.1.%d" % (l, odd)] + four("dh" + L), ["x1%d.%d.%d" % (l, odd, a)])
         o = 512 * (1 - odd)
+        for i, (a, z) in enumerate(pieces):
+            scaled("V" if i < CFG["lowv"][l][odd] else "S", T["x1" + L][:, n * odd + 16 * a:n * odd + 16 * z],
+                   dh.indirect(T["lu" + L][:, c * (2 * odd + 1) + a:c * (2 * odd + 1) + z]), 1.0, ["lu%d.%d" % (l, odd)] + four("dh" + L),
+                   ["x1%d.%d.%d" % (l, odd, a)])
         for a, z in pieces:
-            tt(T["lt" + L][:, o + 16 * a:o + 16 * z], dh.indirect(T["lu" + L][:, c * odd + a:c * odd + z]), T["x1" + L][:, n * odd + 16 * a:n * odd + 16 * z], A.add,
-               ["lu%d.0.%d" % (l, odd), "x1%d.%d.%d" % (l, odd, a), "lt%d.%d" % (l, 1 - odd)] + four("dh" + L), ["lt%d.%d.%d" % (l, odd, a)])
-        quant(("lw", "lo")[odd] + L, 0, 128, T["lt" + L][:, o:o + 512], ["lt%d.%d.%d" % (l, odd, a) for a, z in pieces], [("lw", "lo")[odd] + L])
+            tt(T["lt" + L][:, o + 16 * a:o + 16 * z], dh.indirect(T["lu" + L][:, 2 * c * odd + a:2 * c * odd + z]),
+               T["x1" + L][:, n * odd + 16 * a:n * odd + 16 * z], A.add,
+               ["lu%d.%d" % (l, odd), "x1%d.%d.%d" % (l, odd, a), "lt%d.%d" % (l, 1 - odd)] + four("dh" + L), ["lt%d.%d.%d" % (l, odd, a)])
+        quant(("lw", "lo")[odd] + L, 64 * l * (1 - odd), 128, T["lt" + L][:, o:o + 512], ["lt%d.%d.%d" % (l, odd, a) for a, z in pieces],
+              [("lw", "lo")[odd] + L])
 
-    def layer(l, odd, b0, out, tok, by):
-        h = (C >> l) // 4
-        a = h if odd else 0
-        r = ["lw%d" % l, "wq", "wsc"] + (["land%d" % l] if odd else [])
+    def layer(l, b0, a, lo, r, out, tok, by):
         for b in range(4):
-            mm(b0 + b, "w_", 128 * b, "lw%d" % l, a, 128, True, True, r)
-        lo = 128 - h if odd else 0
+            mm(b0 + b, "w_", 128 * b, "lw%d" % l, a, 128, True, True, ["lw%d" % l, "wq", "wsc"] + r)
         for b in range(4):
-            scaled(by[b], out(b), bank(b0 + b, lo, lo + h), 0.03125, ["ps%d" % (b0 + b)], ["%s.%d" % (tok, b)])
+            scaled(by[b], out(b), bank(b0 + b, lo, lo + 112), 0.03125, ["ps%d" % (b0 + b)], ["%s.%d" % (tok, b)])
 
     made = ([], [])
 
     def highs(l, a, z):
         n, L, o = C >> l, str(l), 4 * HA[l]
+        c = n // 16
+        odd = a // c
         made[l].append("ht%d.%d" % (l, a))
-        tt(T["ht" + L][:, o + 16 * a:o + 16 * z], T["dh" + L][:, 0:4 * n].indirect(T["lu" + L][:, a:z]), T["x1" + L][:, 16 * a:16 * z], A.subtract,
-           ["lu%d.0.0" % l, "lu%d.0.1" % l, "ht" + L] + four("dh" + L) + ["x1%d.%d.%d" % (l, k, c) for k in range(2) for c in CFG["lows"][l][:-1]],
-           made[l][-1:])
+        tt(T["ht" + L][:, o + 16 * a:o + 16 * z], T["dh" + L][:, 0:4 * n].indirect(T["lu" + L][:, c * odd + a:c * odd + z]), T["x1" + L][:, 16 * a:16 * z],
+           A.subtract, ["lu%d.%d" % (l, odd), "ht" + L] + four("dh" + L) + ["x1%d.%d.%d" % (l, odd, k) for k in CFG["lows"][l][odd][:-1]], made[l][-1:])
 
-    def pack_highs(l):
-        quant("h%d" % l, 0, HW[l], T["ht%d" % l][:], made[l], ["h%d" % l])
-
-    def unpack_highs(l, b0):
+    def pack_highs(l, b0):
         w = HW[l]
+        quant("h%d" % l, 0, w, T["ht%d" % l][:], made[l], ["h%d" % l])
         for b in range(2):
             mm(b0 + b, "e_", 128 * b, "h%d" % l, 0, w, True, True, ["h%d" % l, "e0.%d" % b])
-        for b in range(2):
             scaled("S", T["hd%d" % l][:, w * b:w * b + w], bank(b0 + b, 0, w), 1.0, ["ps%d" % (b0 + b)], ["hd%d.%d" % (l, b)])
 
-    def lay(l, odd, banks):
+    def lay(l, a, banks, first=0):
         for i, k in enumerate(banks):
-            b, s = 2 + i // 2, i % 2
-            mm(k, "e_", 128 * (2 * s + b), "h%d" % l, (HW[l] - 128) * odd, 128, True, False, ["h%d" % l, "e%d.%d" % (s, b)])
+            b, s = 2 + (first + i) // 2, (first + i) % 2
+            mm(k, "e_", 128 * (2 * s + b), "h%d" % l, a, 128, True, False, ["h%d" % l, "e%d.%d" % (s, b)])
 
-    def rise(l, odd, src, r, vb, sb_):
-        n = C >> l
-        h = n // 4
-        lo = 128 - h if odd else HA[l]
+    def rise(l, src, a, lo, ha, r, vb, sb_, out, tok):
         for k, b, first in ((sb_[0], 2, 0), (vb[0], 0, 1), (sb_[1], 2, 0), (sb_[2], 3, 0), (vb[1], 1, 1), (sb_[3], 3, 0)):
-            mm(k, "e_", 128 * b, src, h if odd else 0, 128, first == 1, True, r + ["e0.%d" % b])
-        for i in range(4):
-            b, s = i // 2, i % 2
-            a, o = HW[l] * b + HA[l] + h * odd, 4 * (2 * odd + s) + b
-            tt(T["wn%d" % l][:, o:4 * n:16], bank(vb[b], lo, lo + h), T["hd%d" % l][:, a:a + h], (A.add, A.subtract)[s],
-               ["ps%d" % vb[b], "hd%d.%d" % (l, b)], ["wn%d.%d" % (l, o)])
-            scaled("S", T["wn%d" % l][:, o + 2:4 * n:16], bank(sb_[i], lo, lo + h), 1.0, ["ps%d" % sb_[i]], ["wn%d.%d" % (l, o + 2)])
+            mm(k, "e_", 128 * b, src, a, 128, first == 1, True, r + ["e0.%d" % b])
+        for b in range(4):
+            for s in range(2):
+                o, w = HW[l] * b + ha, ["wn%d.%d.%s%d" % (l, b, tok, s)]
+                if b < 2:
+                    tt(out(b, s), bank(vb[b], lo, lo + 112), T["hd%d" % l][:, o:o + 112], (A.add, A.subtract)[s], ["ps%d" % vb[b], "hd%d.%d" % (l, b)], w)
+                else:
+                    k = sb_[2 * (b - 2) + s]
+                    scaled("S", out(b, s), bank(k, lo, lo + 112), 1.0, ["ps%d" % k], w)
 
-    def fetch(l, out, o, a, w, v, r, tok):
+    def fetch(l, out, o, w, off, r, tok):
         n = C >> l
-        for e, lo, hi in (("V", 0, v), ("S", v, w)):
-            scaled(e, T[out][:, 4 * (o + lo):4 * (o + hi)], T["wn%d" % l][:, 0:4 * n].indirect(T["pu%d" % l][:, (a + lo) // 4:(a + hi) // 4]), 1.0,
-                   ["wn%d.%d" % (l, k) for k in range(16)] + r, [tok + e])
+        for b in (3, 2, 0, 1):
+            scaled("VVSS"[b], T[out][:, 4 * o + b:4 * (o + w):4], T["wn%d" % l][:, n * b:n * b + n].indirect(off), 1.0,
+                   ["wn%d.%d.%s%d" % (l, b, t, s) for t in ("eo", "x")[l] for s in range(2)] + r, ["%s.%d" % (tok, b)])
 
-    hc = CFG["highs"]
     orders(0, "pa", 0, 1, 2, (6, 7, 4, 5))
     lows(0, 1)
-    swap(0, 0, "lo0", "lw0", 128, 112, ["lo0"], ["land0"])
+    swap(0, 0, "lo0", 0, "lw0", 128, 112, ["lo0"], ["land0"])
+    iota(T.tab[:], [[1, H // 4], [H // 4, 2], [H // 2, 2]], 0, 0, ["tab"])
+    zero(T.lt1[:, 224:512], 288, ["lt1.0"])
+    zero(T.lt1[:, 736:1024], 288, ["lt1.1"])
+    zero(T.a2t[:, 0:64], 64, four("a2t"))
+    zero(T.psc1[:, 112:128], 16, ["psc1"])
+    zero(T.ht1[:, 0:64], 64, ["ht1"])
+    zero(T.u1t[:, 448:512], 64, ["u1o"])
+    zero(T.u1t[:, 960:1024], 64, ["u1e"])
     lists(0, 0)
     lows(0, 0)
+    layer(0, 4, 0, 0, [], lambda b: T.a1t[:, b:4 * H:8], "a1e", "SSSS")
     quant("ub_", 0, 128, T.ubt[:], ["ubt"], ["ub_"])
-    layer(0, False, 4, lambda b: T.a1t[:, b:4 * H:8], "a1e", "SSSS")
-    pick("pb", 0, "ub_", 0, 128, T.ofu[:, 0:8], 128, ["ub_", "ofu"], "pb")
-    highs(0, hc[0], hc[1])
-    layer(0, True, 0, lambda b: T.a1t[:, 4 + b:4 * H:8], "a1o", "SVSV")
+    pick("pb", "ub_", ["ub_"])
+    highs(0, 0, 14)
+    highs(0, 14, 28)
+    layer(0, 0, 112, 16, ["land0"], lambda b: T.a1t[:, 4 + b:4 * H:8], "a1o", "SVSV")
     quant("a1", 0, H, T.a1t[:], four("a1e") + four("a1o"), ["a1"])
     orders(1, "pb", 4, 5, 6, (0, 1, 2, 3))
     lows(1, 1)
-    swap(1, 1, "lo1", "lw1", 128, 56, ["lo1"], ["land1"])
+    swap(1, 1, "lo1", 0, "lw1", 8, 56, ["lo1"], ["land1"])
     lists(1, 0)
     lows(1, 0)
-    layer(1, False, 4, lambda b: T.a2t[:, 64 + b:288:4], "a2e", "SSSS")
-    highs(1, 0, 28)
-    units(1, (3,))
-    highs(0, hc[1], hc[2])
-    layer(1, True, 0, lambda b: T.a2t[:, 512 + b:512 + 224:4], "a2o", "SVSV")
-    quant("a2o", 0, 128, T.a2t[:, 512:1024], four("a2o"), ["a2o"])
-    swap(2, 1, "a2o", "a2", 128, 56, ["a2o"], ["land2"])
-    pack_highs(1)
-    quant("a2", 0, 128, T.a2t[:, 0:512], four("a2e"), ["a2"])
-    unpack_highs(1, 0)
-    lay(1, 0, (4, 5, 6, 7))
+    highs(1, 0, 14)
+    highs(1, 14, 28)
+    highs(0, 28, 42)
+    highs(0, 42, 56)
+    layer(1, 0, 8, 0, ["land1"], lambda b: T.a2t[:, 64 + b:512:4], "a2t", "SVSV")
+    quant("a2", 0, 128, T.a2t[:], four("a2t"), ["a2"])
+    swap(2, 1, "a2", 16, "a2", 128, 56, ["a2"], ["land2"])
+    pack_highs(1, 4)
+    lay(1, 0, (0, 1, 2, 3))
     for k in range(2):
-        aslist("pu1", "psc1", 112 * k, T.pr1[:, 1 - k:H:2], 112, ["pr1"], "pu1.%d" % k)
-    rise(1, 0, "a2", ["a2"], (2, 3), (4, 5, 6, 7))
-    lay(1, 1, (4, 5, 6, 7))
-    highs(0, hc[2], hc[3])
-    aslist("pu0", "psc0", H, T.pr0[:, H:C], H, ["pr0"], "pu0.1")
-    pack_highs(0)
-    rise(1, 1, "a2", ["a2", "land2"], (2, 3), (4, 5, 6, 7))
-    fetch(1, "u1t", 0, 0, 112, 56, ["pu1.0", "u1o"], "u1o")
-    quant("u1o", 0, 128, T.u1t[:, 0:512], ["u1oV", "u1oS"], ["u1oq"])
-    swap(3, 0, "u1o", "u1", 128, 112, ["u1oq"], ["land3"])
-    lay(0, 0, (4, 5, 6, 7))
-    fetch(1, "u1t", 128, 112, 112, 56, ["pu1.1", "u1e"], "u1e")
-    unpack_highs(0, 0)
-    quant("u1", 0, 128, T.u1t[:, 512:1024], ["u1eV", "u1eS"], ["u1"])
-    aslist("pu0", "psc0", 0, T.pr0[:, 0:H], H, ["pr0"], "pu0.0")
-    rise(0, 0, "u1", ["u1"], (2, 3), (4, 5, 6, 7))
-    lay(0, 1, (0, 1, 4, 5))
+        scan(T.psc1[:, 128 * k:128 * k + 112], k2(112), T.pr1[:, 1 - k:H:2], A.add, A.max, ["k2", "pr1"], ["psc1.%d" % k])
+    ts(T.pu1[:, 0:15], T.psc1[:, 15:240:16], col(10), None, A.add, None, ["psc1", "psc1.0", "psc1.1", "pf10"], ["pu1"])
+    pack_highs(0, 6)
+    rise(1, "a2", 56, 16, 16, ["a2", "land2"], (4, 5), (0, 1, 2, 3), lambda b, s: T.wn1[:, H * b + 112 * s:H * b + 112 * s + 112], "x")
+    lay(0, 96, (6, 7))
+    fetch(1, "u1t", 0, 112, T.pu1[:, 0:7], ["pu1", "u1o"], "u1o")
+    quant("u1o", 0, 128, T.u1t[:, 0:512], four("u1o"), ["u1oq"])
+    swap(3, 0, "u1o", 0, "u1", 128, 112, ["u1oq"], ["land3"])
+    lay(0, 0, (0, 1, 2, 3))
+    fetch(1, "u1t", 128, 112, T.pu1[:, 8:15], ["pu1", "u1e"], "u1e")
+    quant("u1", 0, 128, T.u1t[:, 512:1024], four("u1e"), ["u1"])
     quant("v_", 0, 128, T.vt[:], ["vt"], ["v_"])
-    rise(0, 1, "u1", ["u1", "land3"], (2, 3), (0, 1, 4, 5))
-    parts, a = [], 0
-    for w, v in CFG["parts"]:
-        parts.append((a, w, v))
-        a += w
+    rise(0, "u1", 0, 0, 0, ["u1"], (4, 5), (0, 1, 2, 3), lambda b, s: T.wn0[:, C * b + s:C * b + C:4], "e")
+    lay(0, 96, (0, 1), 2)
+    rise(0, "u1", 112, 16, 112, ["u1", "land3"], (4, 5), (6, 7, 0, 1), lambda b, s: T.wn0[:, C * b + 2 + s:C * b + C:4], "o")
+    todo = CFG["end"].split()
 
-    def store(h):
-        a, w, v = parts[h]
-        scaled("S", T.yt[:, a:a + w], bank(h, 0, w), 1.0, ["ps%d" % h], ["yt%d" % h])
-        dma("S" if h == len(parts) - 1 else "Y", T.y[:, a:a + w], T.yt[:, a:a + w], ["yt%d" % h], [])
+    def stores(h):
+        while todo:
+            k, i, e = todo[0][0], int(todo[0][1]), todo[0][2]
+            if (i if k == "c" else 1) > h:
+                return
+            todo.pop(0)
+            a = H * i
+            if k == "s":
+                dma(e, T.osc[4 * i:4 * i + 4, 0:C], T.u0s[32 * i:32 * i + 4, 0:C], ["u0.0", "u0.1"], [])
+            elif k == "c":
+                dma(e, T.oc[:, 4 * a:4 * (a + H)], T.u0q[:, a:a + H].bitcast(dt.uint8), ["u0.%d" % i], [])
+            else:
+                scaled(CFG["yc"][i], T.yt[:, a:a + H], bank(2 + i, 0, H), 1.0, ["ps%d" % (2 + i)], ["yt%d" % i])
+                dma(e, T.y[:, a:a + H], T.yt[:, a:a + H], ["yt%d" % i], [])
 
-    for h, (a, w, v) in enumerate(parts):
-        fetch(0, "u0t", a, a, w, v, ["pu0.0", "pu0.1"], "u0t%d" % h)
-        quant("u0", a, w, T.u0t[:, 4 * a:4 * (a + w)], ["u0t%dV" % h, "u0t%dS" % h], ["u0.%d" % h])
-        mm(h, "v_", 0, "u0", a, w, True, True, ["v_", "u0.%d" % h])
-        dma("Y", T.oc[:, 4 * a:4 * (a + w)], T.u0q[:, a:a + w].bitcast(dt.uint8), ["u0.%d" % h], [])
-        if h > 0:
-            store(h - 1)
-    for k in range(4):
-        dma("Y", T.osc[4 * k:4 * k + 4, 0:C], T.u0s[32 * k:32 * k + 4, 0:C], ["u0.%d" % h for h in range(len(parts))], [])
-    store(len(parts) - 1)
+    for h in range(2):
+        a = H * h
+        fetch(0, "u0t", a, H, T.ru[:, a // 16:(a + H) // 16], ["ru0"], "u0t%d" % h)
+        quant("u0", a, H, T.u0t[:, 4 * a:4 * (a + H)], four("u0t%d" % h), ["u0.%d" % h])
+        mm(2 + h, "v_", 0, "u0", a, H, True, True, ["v_", "u0.%d" % h])
+        stores(h)
+    for i in ORDER:
+        calls[i]()
     for sem, val in total.items():
         g.wait_ge(T.sem[sem], val)

from concourse.mybir import dt, AluOpType, ActivationFunctionType

A = AluOpType
F = ActivationFunctionType
C = 448
H = C // 2
BIG = 2.0 ** 96
STEP = 1024.0
LOW = -224.0
HW = (224, 128)
HA = (0, 16)
BF, F32, I32, U16, Q8, U8 = "bfloat16", "float32", "int32", "uint16", "float8_e4m3fn_x4", "uint8"
CFG = {
    "rows": (([9, 10, 5, 8, 12], [11, 14, 3, 20, 13, 15, 21, 19, 6], [7, 2]), ([], [7, 6], [5, 8, 4, 2])),
    "plan": ("c25 c27 d c23 c26 c17 s26 c24 s25 e c22 q0 c16 s22 r c4 c1 s24 s4 s1 s27 c18 q4 s18 s16 s23 s17 b q1 q2 q3 q5 q6 a x X",
             "c3 c1 d c12 c10 s12 c9 e c11 c13 s9 s3 s1 s10 s11 s13 r b q0 q1 q2 q3 a x X"),
    "lows": (((0, 10, 20, 28), (0, 6, 16, 28)), ((0, 8, 14), (0, 6, 14))),
    "lowv": ((0, 1), (0, 1)),
    "end": "c0Y c1Y s0Y y0Y s1Y s2Y s3Y y1S",
    "yc": "VS",
}
ORDER = [
    1, 0, 2, 7, 8, 9, 10, 12, 25, 26, 27, 28, 29, 30, 31, 32, 33, 34, 35, 37, 38, 39, 64, 11, 22, 57, 23, 56, 24, 49, 58, 60, 50, 63, 52, 36, 53, 48,
    59, 51, 54, 3, 4, 77, 5, 61, 6, 62, 78, 65, 14, 17, 79, 66, 82, 72, 70, 67, 75, 68, 133, 134, 84, 80, 69, 15, 18, 19, 16, 20, 92, 73, 74, 95, 90,
    76, 71, 121, 118, 119, 81, 117, 124, 93, 89, 21, 13, 40, 41, 45, 94, 100, 91, 97, 120, 85, 86, 87, 88, 128, 129, 139, 122, 126, 140, 44, 103, 102,
    141, 43, 98, 96, 105, 46, 101, 136, 127, 130, 147, 135, 123, 145, 149, 148, 99, 106, 150, 104, 108, 47, 109, 175, 142, 144, 151, 125, 107, 152,
    110, 55, 137, 83, 143, 153, 111, 155, 132, 138, 131, 42, 176, 154, 113, 156, 354, 146, 158, 179, 157, 177, 116, 200, 159, 160, 161, 112, 115, 114,
    217, 163, 162, 165, 183, 202, 164, 182, 166, 168, 184, 167, 169, 171, 186, 170, 185, 216, 187, 172, 189, 174, 173, 190, 188, 191, 201, 195, 199,
    192, 193, 194, 196, 197, 198, 204, 203, 205, 208, 207, 209, 206, 211, 212, 210, 213, 214, 222, 215, 294, 218, 220, 223, 219, 225, 238, 221, 224,
    243, 242, 226, 227, 231, 228, 229, 230, 233, 234, 235, 232, 236, 237, 240, 245, 244, 250, 253, 251, 248, 246, 260, 261, 249, 262, 264, 266, 239,
    263, 265, 241, 267, 252, 256, 257, 255, 254, 258, 247, 259, 269, 268, 270, 271, 272, 273, 316, 277, 274, 275, 285, 284, 276, 286, 278, 279, 288,
    287, 315, 280, 281, 282, 290, 289, 181, 180, 178, 283, 291, 292, 317, 293, 298, 297, 296, 302, 299, 300, 301, 303, 306, 304, 307, 309, 310, 311,
    312, 295, 318, 321, 322, 319, 313, 320, 308, 338, 314, 337, 305, 326, 324, 335, 323, 325, 327, 330, 328, 329, 333, 347, 334, 331, 332, 336, 341,
    340, 342, 346, 348, 345, 339, 352, 343, 350, 349, 351, 344, 353, 355, 356, 357, 365, 359, 360, 358, 361, 362, 366, 369, 367, 363, 364, 370, 368,
    372, 371, 381, 375, 373, 374, 376, 382, 383, 377, 378, 384, 386, 379, 380, 394, 387, 385, 388, 395, 393, 392, 389, 396, 390, 391, 397, 398, 399,
    400, 401, 402, 403, 404, 405, 406]


def _tiles(n):
    segs = ["d"] + list(range(n // 16 - 1, 0, -1))
    out = []
    for u in range(0, len(segs), 4):
        s = segs[u:u + 4]
        out.append((max(128, n if u == 0 else 16 * s[0]), s))
    return out


def _scratch():
    s = {}

    def sb(name, cols, d):
        s[name] = ("sbuf", [128, cols], d)

    def mx(name, cols):
        sb(name + "q", cols, Q8)
        sb(name + "s", cols, U8)
    sb("xt", 4 * C, BF); sb("uat", 512, BF); sb("ubt", 512, BF); sb("vt", 512, BF)
    mx("a0", C); mx("a1", H); mx("ua_", 128); mx("ub_", 128); mx("v_", 128); mx("pa", 128); mx("pb", 128); mx("w_", 512)
    sb("pi", 16, I32); sb("pf", 16, F32); sb("ofu", 8, U16)
    sb("jm", H, BF); sb("jn", 128, BF); sb("jq", 3 * H, BF); sb("one", 512, BF); sb("jj", C, F32); sb("ct", 64, F32)
    sb("kk", 4 * H + C, BF)
    sb("gt", 512, BF); sb("et", 2 * 520, BF); mx("g_", 128); mx("e_", 6 * 128)
    sb("ms", C, F32); sb("cf", C, F32); sb("tmp", 4 * C, BF); sb("dsc", C, BF); sb("csc", C, F32)
    sb("rk", 64, F32); sb("ru", 64, U16); sb("rs", 64, F32)
    sb("a1t", 2 * C, BF); sb("a2t", 512, BF); mx("a2", 184)
    sb("tab", H, F32); sb("pr1", H, F32); sb("psc1", 240, F32); sb("pu1", 16, U16)
    sb("u1t", 1024, BF); mx("u1", 240); mx("u1o", 128)
    sb("u0t", 4 * C, BF); mx("u0", C); sb("yt", C, F32)
    for l in range(2):
        n = C >> l
        w = sum(t[0] for t in _tiles(n))
        L = str(l)
        sb("fl" + L, 4 * w, BF); mx("fl" + L, w); sb("sc" + L, n // 2 * (n // 16), BF)
        sb("oo" + L, n, F32); sb("lsc" + L, n, F32); sb("lu" + L, n // 4, U16); sb("dh" + L, 4 * n, BF); sb("x1" + L, 2 * n, BF)
        sb("lt" + L, 1024, BF); mx("lo" + L, 128); mx("lw" + L, (240, 192)[l])
        sb("ht" + L, 4 * HW[l], BF); mx("h" + L, HW[l]); sb("hd" + L, 2 * HW[l], BF); sb("wn" + L, 4 * n, BF)
    s["ps"] = ("psum", [128, 4096], F32)
    return s


SCRATCH = _scratch()
SEMAPHORES = ["V", "S", "P", "G", "sent"] + ["arr%d" % k for k in range(4)] + ["d%d" % k for k in range(24)]


def rank_program(g, core, T, topo):
    rank = T.rank_of(core)
    if rank is None:
        return
    Q = {"V": g.vector, "S": g.scalar, "P": g.tensor, "G": g, "Y": g.sync}
    total = {}
    seen = {e: {} for e in Q}
    wrote, read = {}, {}
    ndma = [0]
    calls = []

    def need(e, r, w):
        want = {}

        def add(sem, val, who):
            if not (e == "P" and who == "P"):
                want[sem] = max(want.get(sem, 0), val)
        for t in list(r) + list(w):
            if t in wrote:
                add(*wrote[t])
        for t in w:
            for sem, (val, who) in read.get(t, {}).items():
                add(sem, val, who)
        for t in r:
            if t.startswith("ps"):
                for sem, (val, who) in read.get(t, {}).items():
                    if who != e:
                        add(sem, val, who)
        for sem, val in want.items():
            if seen[e].get(sem, 0) < val:
                Q[e].wait_ge(T.sem[sem], val)
                seen[e][sem] = val

    def mark(sem, e, r, w):
        for t in r:
            read.setdefault(t, {})[sem] = (total[sem], e)
        for t in w:
            wrote[t] = (sem, total[sem], e)
            read[t] = {}

    def op(e, fn, r, w):
        def issue():
            need(e, r, w)
            fn().then_inc(T.sem[e], 1)
            total[e] = total.get(e, 0) + 1
            mark(e, e, r, w)
        calls.append(issue)

    def dma(e, out, in_, r, w):
        def issue():
            need(e, r, w)
            sem = "d%d" % ndma[0]
            ndma[0] += 1
            Q[e].dma_start(out, in_).then_inc(T.sem[sem], 16)
            total[sem] = 16
            mark(sem, "dma", r, w)
        calls.append(issue)

    def swap(k, l, src, a, dst, b, cols, r, w):
        def issue():
            peer = T.cores[rank ^ (1 << l)]
            rid, pid = topo.addr(peer)[:2]
            m, sem = topo.mask(core, peer), "arr%d" % k
            need("G", r, [])
            g.remote_dma(T[dst + "q"][:, b:b + cols].bitcast(dt.uint8), T[src + "q"][:, a:a + cols].bitcast(dt.uint8), T.sem[sem], T.sem.sent, pid, rid, m)
            g.remote_dma(T[dst + "s"][:, b:b + cols], T[src + "s"][:, a:a + cols], T.sem[sem], T.sem.sent, pid, rid, m)
            total["sent"] = total.get("sent", 0) + 2 * len(topo.engines(core, peer))
            total[sem] = 2 * len(topo.engines(peer, core))
            mark(sem, "far", [], w)
        calls.append(issue)

    V, S, PE = g.vector, g.scalar, g.tensor

    def bank(b, a, z):
        return T.ps[:, 512 * b + a:512 * b + z]

    def four(name):
        return ["%s.%d" % (name, b) for b in range(4)]

    def quant(dst, a, n, src, r, w):
        op("V", lambda: V.quantize_mx(T[dst + "q"][:, a:a + n], T[dst + "s"][:, a:a + n], src), r, w)

    def mm(b, st, sa, mv, a, n, start, stop, r):
        op("P", lambda: PE.matmul_mx(bank(b, 0, n), T[st + "q"][:, sa:sa + 128], T[st + "s"][:, sa:sa + 128],
                                     T[mv + "q"][:, a:a + n], T[mv + "s"][:, a:a + n], start, stop), r, ["ps%d" % b])

    def ts(out, in0, s1, s2, o0, o1, r, w):
        if s2 is None:
            op("V", lambda: V.tensor_scalar(out, in0, s1, None, o0), r, w)
        else:
            op("V", lambda: V.tensor_scalar(out, in0, s1, s2, o0, o1), r, w)

    def tt(out, in0, in1, o, r, w):
        op("V", lambda: V.tensor_tensor(out, in0, in1, o), r, w)

    def scan(out, d0, d1, o0, o1, r, w, first=0.0):
        op("V", lambda: V.tensor_tensor_scan(out, d0, d1, first, o0, o1), r, w)

    def cp(out, in_, r, w):
        op("V", lambda: V.tensor_copy(out, in_), r, w)

    def fill(ap, val, w):
        op("V", lambda: V.memset(ap, val), [], w)

    def act(out, in_, f, r, w, **kw):
        op("S", lambda: S.activation(out, in_, f, **kw), r, w)

    def scaled(e, out, in_, c, r, w):
        if e == "V":
            if c == 1.0:
                cp(out, in_, r, w)
            else:
                ts(out, in_, c, None, A.mult, None, r, w)
        elif c == 1.0:
            act(out, in_, F.Copy, r, w)
        else:
            act(out, in_, F.Copy, r, w, scale=c)

    def pick(dst, src, r):
        off = T.ofu[:, 0:8]
        cp(T[dst + "q"][:].bitcast(dt.uint32), T[src + "q"][:].bitcast(dt.uint32).indirect(off), r + ["ofu"], [dst + "q"])
        act(T[dst + "s"][:], T[src + "s"][:].indirect(off), F.Copy, r + ["ofu"], [dst + "s"])

    def iota(out, pattern, base, cm, w, small=True):
        if small:
            op("G", lambda: g.iota(out, pattern, base, cm, allow_small_or_imprecise_dtypes=True), [], w)
        else:
            op("G", lambda: g.iota(out, pattern, base, cm), [], w)

    def zero(ap, n, w):
        iota(ap, [[0, n]], 0, 0, w)

    def col(k):
        return T.pf[:, k:k + 1]

    def slots(l, u):
        return four("fl%d.%d" % (l, u)) + (["fl0.0.4"] if l == 0 and u == 0 else [])

    def zero_flags(l, us, how):
        tiles = _tiles(C >> l)
        for u in us:
            w, s = tiles[u]
            a, lo = sum(t[0] for t in tiles[:u]), 0 if len(s) < 4 else 16 * s[-1]
            how(T["fl%d" % l][:, 4 * (a + lo):4 * (a + w)], 4 * (w - lo), slots(l, u))

    def ends(l):
        h = C >> (l + 1)
        return T["sc%d" % l][:, h - 1:h * (h // 8):h]

    def units(kind, bs):
        for b in bs:
            quant("e_", 128 * (2 * kind + b), 128, T.et[:, 520 * kind + 3 - b:520 * kind + 515 - b], ["et%d" % kind], ["e%d.%d" % (kind, b)])

    dma("Y", T.uat[:], T.ua[:], [], ["uat"])
    dma("S", T.xt[:, 0:4 * H], T.x[:, 0:4 * H], [], ["xt0"])
    dma("Y", T.xt[:, 4 * H:4 * C], T.x[:, 4 * H:4 * C], [], ["xt1"])
    dma("Y", T.ubt[:], T.ub[:], ["xt0", "xt1"], ["ubt"])
    dma("Y", T.w_q[:].bitcast(dt.uint8), T.wc[:], [], ["wq"])
    dma("Y", T.w_s[:], T.ws[:], [], ["wsc"])
    dma("Y", T.vt[:], T.v[:], [], ["vt"])

    iota(T.pi[:, 0:1], [[0, 1]], 0, 1, ["pi"], False)
    iota(col(1), [[0, 1]], 0, 1, ["pf1"])
    iota(T.jn[:], [[1, 128]], 0, 0, ["jn"])
    iota(T.pi[:, 8:16], [[16, 8]], 0, 0, ["ofi"], False)
    iota(T.jm[:], [[0, H // 16], [1, 16]], 0, 0, ["jm"])
    fill(T.one[:], 1.0, ["one"])
    iota(T.ct[:, 0:28], [[16, 28]], int(LOW), 0, ["ct"])
    op("G", lambda: g.affine_select(T.gt[:], T.one[:], [[-16, 8], [0, 64]], A.is_ge, 0.0, 0, 1), ["one"], ["gt"])
    op("G", lambda: g.affine_select(T.gt[:], T.gt[:], [[16, 8], [0, 64]], A.is_ge, 0.0, 15, -1), ["gt"], ["gt"])
    zero_flags(0, (3, 6, 2, 1), zero)
    iota(T.jj[:], [[1, C]], 0, 0, ["jj"])
    iota(T.jq[:, 0:H], [[0, H // 4], [1, 4]], 0, 0, ["jq"])

    def wipe(ap, n, w):
        act(ap, T.one[:, 0:n], F.Copy, ["one"], w, scale=0.0)

    zero_flags(0, (4, 5, 0), wipe)
    ts(T.pi[:, 1:2], T.pi[:, 0:1], 15, None, A.bitwise_and, None, ["pi"], ["pj0"])
    fill(T.et[:, 0:516], 0.0, ["et0"])
    cp(col(0), T.pi[:, 1:2], ["pj0"], ["pf"])
    ts(T.et[:, 3:515:4], T.jn[:], col(1), None, A.is_equal, None, ["jn", "pf1"], ["et0"])
    ts(col(3), col(0), -BIG, None, A.mult, None, ["pf"], ["pf3"])
    ts(col(4), col(0), 1.0, BIG, A.add, A.mult, ["pf"], ["pf4"])
    cp(T.ofu[:, 0:8], T.pi[:, 8:16], ["ofi"], ["ofu"])
    ts(T.pi[:, 2:3], T.pi[:, 0:1], 12, None, A.bitwise_and, None, ["pi"], ["pj1"])
    ts(col(6), col(0), -15.0, STEP - 1.0, A.add, A.mult, ["pf"], ["pf6"])
    ts(col(9), T.pi[:, 2:3], STEP - 1.0, col(0), A.mult, A.add, ["pj1", "pf"], ["pf9"])
    fill(T.rs[:], 0.0, ["rs"])
    ts(col(7), T.pi[:, 2:3], 4.0, BIG / 4, A.add, A.mult, ["pj1"], ["pf7"])
    fill(ends(0), LOW, ["sc0"])
    units(0, (2, 3))
    zero(T.lt0[:, 448:512], 64, ["lt0.0"])
    zero(T.lt0[:, 960:1024], 64, ["lt0.1"])
    op("G", lambda: g.affine_select(T.et[:, 520:1036], T.et[:, 0:516], [[1, 516]], A.not_equal, -1.0, -3, -4), ["et0"], ["et1"])
    zero_flags(1, range(4), zero)
    iota(ends(1), [[0, 14]], int(LOW), 0, ["sc1"])

    mz, kr, kk, k3, k2 = [lambda n, k=k, a=0: T.kk[:, H * k + a:H * k + n] for k in range(5)]
    act(mz(H), T.jm[:], F.Abs, ["jm", "pf3"], ["mz"], scale=BIG, bias=col(3))
    act(kr(H), T.jm[:], F.Relu, ["jm", "pf4"], ["kr"], scale=-BIG, bias=col(4))
    quant("ua_", 0, 128, T.uat[:], ["uat"], ["ua_"])
    act(kk(H), kr(H), F.Copy, ["kr"], ["kk"], scale=-1.0)
    pick("pa", "ua_", ["ua_"])
    act(k3(H), T.jm[:], F.Sign, ["jm"], ["k3"])
    act(T.ct[:, 32:60], T.ct[:, 0:28], F.Identity, ["ct", "pf6"], ["cst"], bias=col(6))
    act(col(8), col(9), F.Identity, ["pf9"], ["pf8"], bias=-12 * STEP)
    act(col(10), col(0), F.Identity, ["pf"], ["pf10"], scale=STEP, bias=-15 * STEP)
    act(k2(H), kr(H), F.Identity, ["kr"], ["k2"], scale=-1.0, bias=STEP)
    act(k2(C, a=H), kr(H), F.Identity, ["kr"], ["k2b"], scale=-1.0, bias=STEP)

    def orders(l, st, bv, bs, bx, bd):
        n, L = C >> l, str(l)
        nt, a_, z = n // 16, "a" + L, 32 * l
        fl, rs, rk, sc = T["fl" + L], T.rs, T.rk[:, z:z + nt], T["sc" + L]
        early, main, late = CFG["rows"][l]
        tiles = _tiles(n)
        where, start, a = {}, [], 0
        for u, (w, s) in enumerate(tiles):
            start.append(a)
            for k, t in enumerate(s):
                where[t] = (u, k)
            a += w
        stat = [st + "q", st + "s"]
        atok = ["a0.0", "a0.1"] if l == 0 else ["a1"]
        cut = H if l == 0 else 16 * (main[0] + 1)

        def cft(t):
            return "cfb" if 16 * t >= cut else "cfa"

        def slot(t, lo, hi):
            u, k = where[t]
            return fl[:, 4 * (start[u] + lo) + k:4 * (start[u] + hi):4]

        def stok(t):
            return "fl%d.%d.%d" % ((l,) + where[t])

        def own(b, lo, hi, tok, between=None):
            tt(T.ms[:, lo:hi], bank(b, lo, hi), mz(hi - lo), A.subtract, ["ps%d" % b, "mz"], ["ms" + tok])
            if between:
                between()
            scan(T.cf[:, lo:hi], kk(hi - lo), T.ms[:, lo:hi], A.add, A.max, ["kk", "ms" + tok], ["cf" + tok])

        def inside(b, lo, hi, r, tok):
            tt(slot("d", lo, hi), bank(b, lo, hi), T.cf[:, lo:hi], A.is_le, ["ps%d" % b] + r, [tok])

        def inside_sum(lo, hi, tok):
            scan(T.dsc[:, lo:hi], k3(hi - lo), slot("d", lo, hi), A.mult, A.add, ["k3", tok], ["dsc%d" % (lo > 0)])

        turn = [0]

        def srows(b, rows):
            for i in range(len(rows) + 1):
                if i < len(rows):
                    t, k = rows[i], (turn[0] + i) % 4
                    act(T.tmp[:, C * k:C * k + 16 * t], bank(b, 0, 16 * t), F.Sign, ["ps%d" % b, cft(t)], ["tmp%d" % k],
                        bias=T.cf[:, 16 * t + 15:16 * t + 16], scale=-1.0)
                if i > 0:
                    t, k = rows[i - 1], (turn[0] + i - 1) % 4
                    act(slot(t, 0, 16 * t), T.tmp[:, C * k:C * k + 16 * t], F.Relu, ["tmp%d" % k, "rs"],
                        [stok(t), "rs%d.%d" % (l, t)], accum_out=rs[:, z + t:z + t + 1])
            turn[0] += len(rows)

        if l == 0:
            quant("a0", 0, H, T.xt[:, 0:4 * H], ["xt0"], ["a0.0"])
            mm(bd[2], st, 0, a_, 0, H, True, True, ["a0.0"] + stat)
            mm(bd[3], st, 0, a_, 0, H, True, True, ["a0.0"] + stat)
            units(0, (0, 1))
            own(bd[2], 0, H, "a")
            srows(bd[3], early)
            quant("a0", H, H, T.xt[:, 4 * H:4 * C], ["xt1"], ["a0.1"])
            mm(bv, st, 0, a_, 0, n, True, True, atok + stat)
            mm(bs, st, 0, a_, 0, n, True, True, atok + stat)
            inside(bd[2], 0, H, ["cfa"], "fl0.0.0")
            quant("g_", 0, 128, T.gt[:], ["gt"], ["g_"])
            own(bv, H, n, "b", lambda: inside_sum(0, H, "fl0.0.0"))
            dl, dtok = H, "fl0.0.4"
        else:
            mm(bv, st, 0, a_, 0, n, True, True, atok + stat)
            mm(bs, st, 0, a_, 0, n, True, True, atok + stat)
            units(1, (2, 3))
            own(bv, 0, cut, "a")
            own(bv, cut, n, "b")
            dl, dtok = 0, "fl1.0.0"
        for b in range(4):
            mm(bd[b], "e_", 128 * b, a_, 0, n, True, True, atok + ["e0.%d" % b])
        srows(bs, main + late)
        if l == 0:
            act(T.jq[:, H:2 * H], T.jq[:, 0:H], F.Relu, ["jq", "pf7"], ["kq"], scale=-BIG, bias=col(7))
        for b in range(4):
            scaled("S", T["dh" + L][:, b:4 * n:4], bank(bd[b], 0, n), 0.5, ["ps%d" % bd[b]], ["dh%d.%d" % (l, b)])
            if l == 0 and b == 0:
                act(T.jq[:, 2 * H:3 * H], T.jq[:, H:2 * H], F.Identity, ["kq"], ["k4"], scale=-1.0, bias=STEP)
        plan = [(w[0], int(w[1:] or 0)) for w in CFG["plan"][l].split()]
        rows = [t for k, t in plan if k == "c"]
        shut, held = [u for k, u in plan if k == "q"], []
        turns = [0] + [u for u in shut if u != 0]
        for k, t in plan:
            if k == "d":
                inside(bv, dl, n, ["cfa", "cfb"], dtok)
            elif k == "e":
                inside_sum(dl, n, dtok)
            elif k == "c":
                ts(slot(t, 0, 16 * t), bank(bv, 0, 16 * t), T.cf[:, 16 * t + 15:16 * t + 16], None, A.is_lt, None, ["ps%d" % bv, cft(t)], [stok(t)])
            elif k == "s":
                e = n // 2 * (t + 1)
                scan(sc[:, e - 8 * t:e], slot(t, 0, 8 * t), slot(t, 8 * t, 16 * t), A.add, A.add, [stok(t), "sc" + L], ["sc%d.%d" % (l, t)], LOW)
            elif k == "r":
                tt(rk, T.ct[:, 32:32 + nt], T.dsc[:, 15:n:16], A.subtract, ["cst", "dsc0", "dsc1"], ["rk" + L])
            elif k == "a":
                tt(rk, rk, rs[:, z:z + nt], A.subtract, ["rk" + L, "rs"] + ["rs%d.%d" % (l, t) for t in early + main + late], ["rk" + L])
            elif k == "b":
                tt(rk, rk, ends(l), A.subtract, ["rk" + L] + ["sc%d.%d" % (l, t) for t in rows], ["rk" + L])
            elif k == "x":
                scan(T.csc[:, 0:n], k2(n), bank(bx, 0, n), A.add, A.max, ["k2", "k2b", "ps%d" % bx], ["csc"])
            elif k == "X":
                tt(rk, rk, T.csc[:, 15:n:16], A.add, ["csc", "rk" + L], ["rk" + L])
            else:
                quant("fl" + L, start[t], tiles[t][0], fl[:, 4 * start[t]:4 * (start[t] + tiles[t][0])], slots(l, t), ["flq%d.%d" % (l, t)])
                held.append(t)
                if 0 in shut[:shut.index(t) + 1]:
                    for v in [v for v in turns if v in held]:
                        held.remove(v)
                        mm(bx, "g_", 0, "fl" + L, start[v], tiles[v][0], v == 0, v == turns[-1], ["g_", "flq%d.%d" % (l, v)])
        cp(T.ru[:, z:z + nt], rk, ["rk" + L], ["ru" + L])
        cp(T["oo" + L][:, 0:n].indirect(T.ru[:, z:z + nt]), T.jj[:, 0:n], ["ru" + L, "jj"], ["oo" + L])
        if l == 1:
            act(T.pr1[:], T.tab[:].indirect(T.ru[:, z:z + nt]), F.Copy, ["ru1", "tab"], ["pr1"])
        lists(l, 1)
        dma("Y", T.ol[0:8, l * C:l * C + n], T["oo" + L][0:128:16, 0:n], ["oo" + L], [])

    def lists(l, odd):
        n, L = C >> l, str(l)
        a, m, tok = n // 2 * odd, n // 4, "lu%d.%d" % (l, odd)
        for k in range(2):
            scan(T["lsc" + L][:, a + k * m:a + k * m + m], T.jq[:, 2 * H:2 * H + m], T["oo" + L][:, 2 * odd + k:n:4], A.add, A.max,
                 ["k4", "oo" + L], ["%s.%d" % (tok, k)])
        ts(T["lu" + L][:, a // 4:(a + 2 * m) // 4], T["lsc" + L][:, a + 3:a + 2 * m:4], 4.0, col(8), A.mult, A.add, [tok + ".0", tok + ".1", "pf8"], [tok])

    def lows(l, odd):
        n, L = C >> l, str(l)
        c, cuts, dh = n // 16, CFG["lows"][l][odd], T["dh" + L][:, 0:4 * n]
        pieces = list(zip(cuts, cuts[1:]))
        o = 512 * (1 - odd)
        for i, (a, z) in enumerate(pieces):
            scaled("V" if i < CFG["lowv"][l][odd] else "S", T["x1" + L][:, n * odd + 16 * a:n * odd + 16 * z],
                   dh.indirect(T["lu" + L][:, c * (2 * odd + 1) + a:c * (2 * odd + 1) + z]), 1.0, ["lu%d.%d" % (l, odd)] + four("dh" + L),
                   ["x1%d.%d.%d" % (l, odd, a)])
        for a, z in pieces:
            tt(T["lt" + L][:, o + 16 * a:o + 16 * z], dh.indirect(T["lu" + L][:, 2 * c * odd + a:2 * c * odd + z]),
               T["x1" + L][:, n * odd + 16 * a:n * odd + 16 * z], A.add,
               ["lu%d.%d" % (l, odd), "x1%d.%d.%d" % (l, odd, a), "lt%d.%d" % (l, 1 - odd)] + four("dh" + L), ["lt%d.%d.%d" % (l, odd, a)])
        quant(("lw", "lo")[odd] + L, 64 * l * (1 - odd), 128, T["lt" + L][:, o:o + 512], ["lt%d.%d.%d" % (l, odd, a) for a, z in pieces],
              [("lw", "lo")[odd] + L])

    def layer(l, b0, a, lo, r, out, tok, by):
        for b in range(4):
            mm(b0 + b, "w_", 128 * b, "lw%d" % l, a, 128, True, True, ["lw%d" % l, "wq", "wsc"] + r)
        for b in range(4):
            scaled(by[b], out(b), bank(b0 + b, lo, lo + 112), 0.03125, ["ps%d" % (b0 + b)], ["%s.%d" % (tok, b)])

    made = ([], [])

    def highs(l, a, z):
        n, L, o = C >> l, str(l), 4 * HA[l]
        c = n // 16
        odd = a // c
        made[l].append("ht%d.%d" % (l, a))
        tt(T["ht" + L][:, o + 16 * a:o + 16 * z], T["dh" + L][:, 0:4 * n].indirect(T["lu" + L][:, c * odd + a:c * odd + z]), T["x1" + L][:, 16 * a:16 * z],
           A.subtract, ["lu%d.%d" % (l, odd), "ht" + L] + four("dh" + L) + ["x1%d.%d.%d" % (l, odd, k) for k in CFG["lows"][l][odd][:-1]], made[l][-1:])

    def pack_highs(l, b0):
        w = HW[l]
        quant("h%d" % l, 0, w, T["ht%d" % l][:], made[l], ["h%d" % l])
        for b in range(2):
            mm(b0 + b, "e_", 128 * b, "h%d" % l, 0, w, True, True, ["h%d" % l, "e0.%d" % b])
            scaled("S", T["hd%d" % l][:, w * b:w * b + w], bank(b0 + b, 0, w), 1.0, ["ps%d" % (b0 + b)], ["hd%d.%d" % (l, b)])

    def lay(l, a, banks, first=0):
        for i, k in enumerate(banks):
            b, s = 2 + (first + i) // 2, (first + i) % 2
            mm(k, "e_", 128 * (2 * s + b), "h%d" % l, a, 128, True, False, ["h%d" % l, "e%d.%d" % (s, b)])

    def rise(l, src, a, lo, ha, r, vb, sb_, out, tok):
        for k, b, first in ((sb_[0], 2, 0), (vb[0], 0, 1), (sb_[1], 2, 0), (sb_[2], 3, 0), (vb[1], 1, 1), (sb_[3], 3, 0)):
            mm(k, "e_", 128 * b, src, a, 128, first == 1, True, r + ["e0.%d" % b])
        for b in range(4):
            for s in range(2):
                o, w = HW[l] * b + ha, ["wn%d.%d.%s%d" % (l, b, tok, s)]
                if b < 2:
                    tt(out(b, s), bank(vb[b], lo, lo + 112), T["hd%d" % l][:, o:o + 112], (A.add, A.subtract)[s], ["ps%d" % vb[b], "hd%d.%d" % (l, b)], w)
                else:
                    k = sb_[2 * (b - 2) + s]
                    scaled("S", out(b, s), bank(k, lo, lo + 112), 1.0, ["ps%d" % k], w)

    def fetch(l, out, o, w, off, r, tok):
        n = C >> l
        for b in (3, 2, 0, 1):
            scaled("VVSS"[b], T[out][:, 4 * o + b:4 * (o + w):4], T["wn%d" % l][:, n * b:n * b + n].indirect(off), 1.0,
                   ["wn%d.%d.%s%d" % (l, b, t, s) for t in ("eo", "x")[l] for s in range(2)] + r, ["%s.%d" % (tok, b)])

    orders(0, "pa", 0, 1, 2, (6, 7, 4, 5))
    lows(0, 1)
    swap(0, 0, "lo0", 0, "lw0", 128, 112, ["lo0"], ["land0"])
    iota(T.tab[:], [[1, H // 4], [H // 4, 2], [H // 2, 2]], 0, 0, ["tab"])
    zero(T.lt1[:, 224:512], 288, ["lt1.0"])
    zero(T.lt1[:, 736:1024], 288, ["lt1.1"])
    zero(T.a2t[:, 0:64], 64, four("a2t"))
    zero(T.psc1[:, 112:128], 16, ["psc1"])
    zero(T.ht1[:, 0:64], 64, ["ht1"])
    zero(T.u1t[:, 448:512], 64, ["u1o"])
    zero(T.u1t[:, 960:1024], 64, ["u1e"])
    lists(0, 0)
    lows(0, 0)
    layer(0, 4, 0, 0, [], lambda b: T.a1t[:, b:4 * H:8], "a1e", "SSSS")
    quant("ub_", 0, 128, T.ubt[:], ["ubt"], ["ub_"])
    pick("pb", "ub_", ["ub_"])
    highs(0, 0, 14)
    highs(0, 14, 28)
    layer(0, 0, 112, 16, ["land0"], lambda b: T.a1t[:, 4 + b:4 * H:8], "a1o", "SVSV")
    quant("a1", 0, H, T.a1t[:], four("a1e") + four("a1o"), ["a1"])
    orders(1, "pb", 4, 5, 6, (0, 1, 2, 3))
    lows(1, 1)
    swap(1, 1, "lo1", 0, "lw1", 8, 56, ["lo1"], ["land1"])
    lists(1, 0)
    lows(1, 0)
    highs(1, 0, 14)
    highs(1, 14, 28)
    highs(0, 28, 42)
    highs(0, 42, 56)
    layer(1, 0, 8, 0, ["land1"], lambda b: T.a2t[:, 64 + b:512:4], "a2t", "SVSV")
    quant("a2", 0, 128, T.a2t[:], four("a2t"), ["a2"])
    swap(2, 1, "a2", 16, "a2", 128, 56, ["a2"], ["land2"])
    pack_highs(1, 4)
    lay(1, 0, (0, 1, 2, 3))
    for k in range(2):
        scan(T.psc1[:, 128 * k:128 * k + 112], k2(112), T.pr1[:, 1 - k:H:2], A.add, A.max, ["k2", "pr1"], ["psc1.%d" % k])
    ts(T.pu1[:, 0:15], T.psc1[:, 15:240:16], col(10), None, A.add, None, ["psc1", "psc1.0", "psc1.1", "pf10"], ["pu1"])
    pack_highs(0, 6)
    rise(1, "a2", 56, 16, 16, ["a2", "land2"], (4, 5), (0, 1, 2, 3), lambda b, s: T.wn1[:, H * b + 112 * s:H * b + 112 * s + 112], "x")
    lay(0, 96, (6, 7))
    fetch(1, "u1t", 0, 112, T.pu1[:, 0:7], ["pu1", "u1o"], "u1o")
    quant("u1o", 0, 128, T.u1t[:, 0:512], four("u1o"), ["u1oq"])
    swap(3, 0, "u1o", 0, "u1", 128, 112, ["u1oq"], ["land3"])
    lay(0, 0, (0, 1, 2, 3))
    fetch(1, "u1t", 128, 112, T.pu1[:, 8:15], ["pu1", "u1e"], "u1e")
    quant("u1", 0, 128, T.u1t[:, 512:1024], four("u1e"), ["u1"])
    quant("v_", 0, 128, T.vt[:], ["vt"], ["v_"])
    rise(0, "u1", 0, 0, 0, ["u1"], (4, 5), (0, 1, 2, 3), lambda b, s: T.wn0[:, C * b + s:C * b + C:4], "e")
    lay(0, 96, (0, 1), 2)
    rise(0, "u1", 112, 16, 112, ["u1", "land3"], (4, 5), (6, 7, 0, 1), lambda b, s: T.wn0[:, C * b + 2 + s:C * b + C:4], "o")
    todo = CFG["end"].split()

    def stores(h):
        while todo:
            k, i, e = todo[0][0], int(todo[0][1]), todo[0][2]
            if (i if k == "c" else 1) > h:
                return
            todo.pop(0)
            a = H * i
            if k == "s":
                dma(e, T.osc[4 * i:4 * i + 4, 0:C], T.u0s[32 * i:32 * i + 4, 0:C], ["u0.0", "u0.1"], [])
            elif k == "c":
                dma(e, T.oc[:, 4 * a:4 * (a + H)], T.u0q[:, a:a + H].bitcast(dt.uint8), ["u0.%d" % i], [])
            else:
                scaled(CFG["yc"][i], T.yt[:, a:a + H], bank(2 + i, 0, H), 1.0, ["ps%d" % (2 + i)], ["yt%d" % i])
                dma(e, T.y[:, a:a + H], T.yt[:, a:a + H], ["yt%d" % i], [])

    for h in range(2):
        a = H * h
        fetch(0, "u0t", a, H, T.ru[:, a // 16:(a + H) // 16], ["ru0"], "u0t%d" % h)
        quant("u0", a, H, T.u0t[:, 4 * a:4 * (a + H)], four("u0t%d" % h), ["u0.%d" % h])
        mm(2 + h, "v_", 0, "u0", a, H, True, True, ["v_", "u0.%d" % h])
        stores(h)
    for i in ORDER:
        calls[i]()
    for sem, val in total.items():
        g.wait_ge(T.sem[sem], val)
